import numpy as np, ml_dtypes
CORES = [25,29,65,69,153,157,193,197]
N = 8
import mx_ref
BF = ml_dtypes.bfloat16
def gcols(t, e):
    v = np.concatenate([t.reshape(8, 16, -1, 4), np.zeros((8, 16, 1, 4), BF)], axis=2)
    return np.ascontiguousarray(np.stack([v[g][:, e[g]] for g in range(8)])).reshape(128, -1)
def tile(rs):
    return np.stack(rs, axis=2).reshape(128, -1).astype(BF)
def pick(q, e):
    c = np.concatenate([q[0].reshape(128, -1, 4), np.zeros((128, 1, 4), np.uint8)], axis=1); s = np.concatenate([q[1], np.ones((16, 1), np.uint8)], axis=1)
    return (np.ascontiguousarray(c[:, e].reshape(128, -1)), np.ascontiguousarray(s[:, e]))
def join(*qs):
    return (np.concatenate([q[0] for q in qs], axis=1), np.concatenate([q[1] for q in qs], axis=1))
def put(q, e, v):
    c, s = q[0].reshape(128, -1, 4).copy(), q[1].copy(); c[:, e] = v[0].reshape(128, -1, 4); s[:, e] = v[1]
    return (c.reshape(128, -1), s)
def pk(c, s):
    return (np.ascontiguousarray(c), mx_ref.live(s))
def emit(q):
    return q[0], q[1]
def packed(v, rng):
    q = [mx_ref.quantize(np.ascontiguousarray(v[r])) for r in range(N)]
    return np.stack([a for a, b in q]), np.stack([mx_ref.plane(b, rng) for a, b in q])
def values_of_codes():
    e, c = np.zeros((128, 128, 4), np.float32), np.zeros((128, 2, 4), np.uint8)
    e[np.arange(128), np.arange(128), 0] = 1
    c[:127, :, 0] = np.arange(256).reshape(2, 128).T[:127]
    return mx_ref.matmul(mx_ref.quantize(e.reshape(128, 512).astype(BF)), (c.reshape(128, 8), np.full((16, 2), 127, np.uint8))).T.reshape(-1).astype(np.float64)
CODE_VALUE, SCALE_VALUE = values_of_codes(), 2.0 ** (np.arange(256) - 127.0)
def decode(q):
    return (CODE_VALUE[q[0]].reshape(16, 8, -1, 4) * SCALE_VALUE[q[1]][:, None, :, None] + 0.0).reshape(128, -1).astype(np.float32)
def f(rng, *shape):
    return mx_ref.flush((rng.standard_normal(shape, dtype=np.float32) * np.exp2(rng.integers(-2, 3, shape[:-1] + (1,)))).astype(BF))
def wide(rng, *shape, cols=0):
    v = rng.standard_normal(shape, dtype=np.float32) * np.exp2(rng.integers(-12, 13, shape)).astype(np.float32)
    if cols: v *= np.repeat(np.exp2(rng.integers(-cols, cols + 1, shape[:-2] + (1, shape[-1] // 4))) * (rng.random(shape[:-2] + (1, shape[-1] // 4)) > 0.0625), 4, axis=-1).astype(np.float32)
    return mx_ref.flush(v.astype(BF))
C, CAP = 288, 128
MASK = [1, 2, 4]
def big(v):
    v = v.astype(np.float32)
    v[np.abs(v) < np.float32(2.0 ** -16)] = 0
    return v.astype(BF)
def alike(u):
    return np.stack([np.reshape(u, (128, 512)).astype(np.float32).astype(BF)] * N)
def numbers_of(rng):
    return {"x": big(f(rng, N, 128, 4 * C)), "u": alike(f(rng, 128, 512)), "v": np.array(f(rng, N, 128, 512))}
def parts(d):
    u = d["u"][0].astype(np.float32).reshape(128, 128, 4)
    u[:, ::16] = 0
    u[:, 1::16] = 0
    return d["x"].astype(np.float32).reshape(N, 8, 16, C, 4), u
def back(x):
    return x.astype(np.float32).reshape(N, 128, 4 * C).astype(BF)
def weights(rng, still=[]):
    w = big(f(rng, N, 128, 2048)).reshape(N, 8, 16, 4, 8, 16, 4)
    for i in still:
        w[:, :, i] = 0
        w[:, :, :, :, :, i] = 0
    c, s = packed(w.reshape(N, 128, 2048), rng)
    return {"wc": c, "ws": s}
def setup_inputs(rng):
    return {**numbers_of(rng), **weights(rng)}
def setup_inputs_ties(rng):
    d = numbers_of(rng)
    x, u = parts(d)
    e = rng.permutation(N)
    k = rng.integers(0, 3, (N, 8, C))
    s = rng.integers(-1, 2, (N, 8, C))
    k[e[0]] = 0
    k[e[1]] *= -1
    k[e[3]] = np.arange(C) // 128
    s[e[0]] = 0
    s[e[2]] = 1
    s[e[3]] = -1
    x[:, :, :2] = 0
    x[:, :, 0, :, 0] = k
    x[:, :, 1, :, 0] = s
    for h in range(0, 128, 16):
        u[h, h, 0] = 1
        u[h + 1, h + 1, 0] = 1
    return {"x": back(x), "u": alike(u), "v": d["v"], **weights(rng, [0, 1])}
def setup_inputs_near(rng):
    d = numbers_of(rng)
    x, u = parts(d)
    x[:, :, 0] = 0
    x[:, :, 8:] = 0
    o = rng.permutation(8)
    s = rng.integers(0, 16, (N, 8, C))
    sign = rng.integers(-1, 2, (N, 8, C))
    for g in range(8):
        h, kind = 16 * g, o[g] // 2
        if kind < 3:
            c = 2.0 ** -30 if kind == 2 else 1.0
            x[:, g, 0, :, 0] = 1.0 if kind == 0 else -1.0 if kind == 1 else rng.integers(0, 2, (N, C)) * 2.0 - 1.0
            x[:, g, 8] = ((s[:, g, :, None] >> np.arange(4)) & 1) * np.exp2(np.arange(4) - 23.0)
            x[:, g, 11, :, 0] = 2.0 ** -10
            x[:, g, 9, :, 0] = sign[:, g] * 2.0 ** -23
            u[h, h, 0] = c
            u[h + 8, h] = c
            u[h + 11, h, 0] = c
            u[h + 9, h + 1, 0] = 2.0 ** -30
        else:
            t = s[:, g] // 4 % 2
            x[:, g, 10, :, 0] = np.where(s[:, g] < 8, -1.0, 1.0) * (1.0 + (s[:, g] % 4) * 0.125) * 2.0 ** -30
            x[:, g, 12, :, 0] = -t * (1.25 * 2.0 ** -30)
            x[:, g, 13, :, 0] = t * (1.125 * 2.0 ** -30)
            x[:, g, 9, :, 0] = sign[:, g] * (1.125 * 2.0 ** -30)
            x[:, g, 14, :, 0] = -sign[:, g] * (1.25 * 2.0 ** -30)
            u[h + 10, h, 0] = 2.0 ** -30
            u[h + 12, h, 0] = 2.0 ** -30
            u[h + 13, h, 0] = 1.125 * 2.0 ** -30
            u[h + 9, h + 1, 0] = 1.125 * 2.0 ** -30
            u[h + 14, h + 1, 0] = 2.0 ** -30
        if o[g] % 2:
            for r in range(N): x[r, g, 0 if kind < 3 else 10, rng.integers(C), 0] = 2.0 ** 29 * (rng.integers(0, 2) * 2.0 - 1.0)
    return {"x": back(x), "u": alike(u), "v": d["v"], **weights(rng, [0, 8, 9, 10, 11, 12, 13, 14, 15])}
def setup_inputs_caps(rng):
    d = numbers_of(rng)
    x, u = parts(d)
    k = rng.permutation([0, 1, CAP - 1, CAP, CAP + 1, 257, C - 1, C])
    x[:, :, 0] = 0
    x[:, :, 0, :, 0] = np.where(np.arange(C) < k[:, None], 1.0, -1.0) * (1.0 + 0.125 * rng.integers(0, 8, (N, 8, C)))
    x[:, :, 0, :, 1:3] = rng.integers(-3, 4, (N, 8, C, 2)) * 0.03125
    a = (1.125 + 0.25 * rng.integers(0, 4, (N, 8, C, 32))) * np.exp2(-rng.integers(8, 15, (N, 8, C, 32)).astype(np.float32))
    np.put_along_axis(a, rng.integers(0, 32, (N, 8, C, 1)), 1.96875, axis=3)
    a *= (rng.integers(0, 2, a.shape) * 2.0 - 1.0) * np.exp2(rng.integers(-3, 4, (N, 8, C, 1)).astype(np.float32))
    x[:, :, 8:] = a.reshape(N, 8, C, 8, 4).transpose(0, 1, 3, 2, 4)
    for h in range(0, 128, 16):
        u[h, h, :3] = 1
        u[h, h + 1, 0] = 1
    return {"x": back(x), "u": alike(u), "v": d["v"], **weights(rng, [0])}
def setup_inputs_huge(rng):
    d = numbers_of(rng)
    x, u = parts(d)
    h = rng.permutation(8)
    x = (0.75 + 0.2 * rng.random((N, 8, 16, C, 4))) * 2.0 ** 30
    x[:, h[:4]] *= -1.0
    x[:, h[4:]] *= rng.integers(0, 2, (N, 1, 1, C, 1)) * 2.0 - 1.0
    for i in range(8):
        g = 16 * h[i]
        for a in (h[:4] if i < 2 else h[4:] if i in (4, 5) else h[i:i + 1]): u[16 * a:16 * a + 16, g] = 2.0 ** 30 * (1.0 - 0.1 * rng.random((16, 4)))
        if i == 1:
            for a in h[4:]: u[16 * a:16 * a + 16, g] = 0.875 * 2.0 ** 30 * (1.0 - 0.1 * rng.random((16, 4)))
        a = 16 * h[4 + i % 4]
        u[a:a + 16, g + 1] = 2.0 ** 30 * (1.0 - 0.1 * rng.random((16, 4))) * (rng.integers(0, 2) * 2.0 - 1.0)
    w = np.zeros((N, 128, 4, 128, 4), np.float32)
    i = np.arange(128)
    for b in range(4): w[:, i, b, i, b] = -1
    c, s = packed(w.reshape(N, 128, 2048).astype(BF), rng)
    return {"x": back(x), "u": alike(u), "v": d["v"], "wc": c, "ws": s}
def setup_inputs_spread(rng):
    d = setup_inputs(rng)
    d["x"] = big(wide(rng, N, 128, 4 * C, cols=6))
    return d
def check_inputs(d):
    b = []
    for k in ("x", "u", "v"):
        a = np.abs(d[k].astype(np.float32))
        if not (np.isfinite(a).all() and ((a == 0) | (a >= 2.0 ** -30) & (a <= 2.0 ** 30)).all()): b.append("a value of " + k)
    if (d["u"].astype(np.float32) != d["u"][:1].astype(np.float32)).any(): b.append("u isn't the same on all ranks")
    none, least, most = [emit(mx_ref.quantize(np.full((128, 16), k, np.float32).astype(BF)))[1][0, 0] for k in (0.0, 2.0 ** -30, 2.0 ** 30)]
    for r in range(N):
        if ((d["wc"][r] == 0x7F) | (d["wc"][r] == 0xFF)).any(): b.append("wc: a code that is no number")
        s = mx_ref.live(d["ws"][r])
        if ((s != none) & ((s < least) | (s > most))).any(): b.append("ws: a scale out of range")
    return b
def reference(x, u, v, wc, ws):
    qu = [mx_ref.quantize(u[r]) for r in range(N)]
    lay = [pk(wc[r], ws[r]) for r in range(N)]
    now = [x[r] for r in range(N)]
    before = np.arange(C)[:, None] < np.arange(C)
    for m in MASK:
        q = [mx_ref.quantize(now[r]) for r in range(N)]
        tab, take = np.zeros((N, 8, C), np.int64), np.zeros((N, 8, C), bool)
        for r in range(N):
            s = mx_ref.matmul(qu[r], q[r])
            k = s[::16] + np.float32(0.0)
            tab[r] = np.count_nonzero((k[:, :, None] >= k[:, None, :]) & before, axis=1)
            want = s[1::16] > 0
            np.put_along_axis(take[r], np.argsort(~want, axis=1, kind="stable")[:, :CAP], True, axis=1)
            take[r] &= want
        e = np.arange(N) ^ m
        mixed = np.where(take, tab[e], tab)
        place = np.zeros((N, 8, C), np.int64)
        for i in range(C):
            place[:, :, :i] += place[:, :, :i] >= mixed[:, :, i:i + 1]
            place[:, :, i] = mixed[:, :, i]
        o = np.argsort(place, axis=2, kind="stable")
        name = o + C * np.take_along_axis(take, o, axis=2)
        made = []
        for r in range(N):
            z = gcols(np.concatenate([now[r], decode(q[e[r]]).astype(BF)], axis=1), name[r])
            qz = mx_ref.quantize(z)
            made.append(tile([mx_ref.matmul(pick(lay[r], np.arange(128 * b, 128 * b + 128)), qz) * np.float32(0.03125) + z[:, b::4].astype(np.float32) for b in range(4)]))
        now = made
    y, od = np.zeros((N, 128, C), np.float32), np.zeros((N, 8, C), np.float32)
    oc, osc = np.zeros((N, 128, 4 * C), np.uint8), np.zeros((N, 16, C), np.uint8)
    for r in range(N):
        q = mx_ref.quantize(now[r])
        y[r] = mx_ref.matmul(mx_ref.quantize(v[r]), q)
        od[r] = name[r]
        oc[r], osc[r] = emit(q)
    return {"y": y, "od": od, "oc": oc, "osc": osc}

@@ -1,0 +1,415 @@
+from concourse.bass import DstId, RemoteDMATransfer
+from concourse.mybir import dt, AluOpType, ActivationFunctionType
+
+C, CAP, NB = 288, 128, 18
+MASKS = [1, 2, 4]
+KV = 13
+SEG = 8 * KV * (KV + 1)
+JUNK = 16 - KV
+LO, HI = 16 * KV, C - 16 * KV
+CUT = C - 128
+LM0 = 4
+H = C // 2
+U = 2.0 ** -10
+TOP = 2.0 ** 14
+WIPE = 2.0 ** 25
+OW = C - 16 + 1
+
+F32, BF, F16, U16, I32, Q4, U8 = "float32", "bfloat16", "float16", "uint16", "int32", "float8_e4m3fn_x4", "uint8"
+
+
+def _sb(n, t):
+    return ("sbuf", [128, n], t)
+
+
+SCRATCH = {
+    "ps": ("psum", [128, 4096], F32),
+    "xt": _sb(4 * C, BF), "ut": _sb(512, BF), "vt": _sb(512, BF), "zt": _sb(4 * C, BF), "z32": _sb(4 * C, BF),
+    "win": _sb(8 * C, BF),
+    "uc": _sb(128, Q4), "us": _sb(128, U8), "upc": _sb(256, Q4), "ups": _sb(256, U8),
+    "vc": _sb(128, Q4), "vs": _sb(128, U8), "ec": _sb(512, Q4), "es": _sb(512, U8),
+    "wq": _sb(512, Q4), "wp": _sb(512, U8), "zc": _sb(C, Q4), "zs": _sb(C, U8),
+    "dist": _sb(518, BF), "eb": _sb(1032, BF),
+    "uli": _sb(16, I32), "ul": _sb(16, U16), "pi": _sb(2, I32), "cc": _sb(16, F32), "lists": _sb(4, U16),
+    "iot": _sb(2 * C, F32), "tmp": _sb(C, F32), "tmn": _sb(C, F32), "hot": _sb(C, BF), "keep": _sb(SEG + HI, BF), "keepf": _sb(LO, BF),
+    "mx": _sb(C, F16), "mo": _sb(C, F32), "cap": _sb(C, F16), "iod": _sb(NB, F32),
+    "taba": _sb(2 * C + 1, F32), "tabb": _sb(2 * C + 1, F32), "ca": _sb(C, F32), "cb": _sb(C, F32),
+    "sm": _sb(C, F32), "hs": _sb(C, F32), "cmp": _sb(SEG + HI, BF), "cs": _sb(SEG + HI, BF),
+    "sg": _sb((NB - KV) * C, BF), "sr": _sb((NB - KV) * C, BF), "acc": _sb(NB - KV, F32),
+    "wt": _sb(C, F16), "cum": _sb(C + 2, F16), "e1": _sb(C, F16), "e2": _sb(C, F16),
+    "take": _sb(NB, F32), "n1": _sb(NB, F32), "n2": _sb(NB, F32), "n16": _sb(NB, U16), "name": _sb(C, F32),
+    "p1": _sb(NB, F32), "p2": _sb(NB, F32), "p3": _sb(NB, F32),
+    "mm": _sb(NB, F32), "m16": _sb(NB, U16),
+    "a32": _sb(C, F32), "ad": _sb(C + 1, F32), "bd": _sb(C + 1, F32), "dout": _sb(C, F32),
+    "al": _sb(NB, F32), "bl": _sb(NB, F32), "v1": _sb(NB, F32), "v2": _sb(NB, F32),
+    "a16": _sb(C + 2, F16), "b16": _sb(C + 2, F16), "o16": _sb((NB - 1) * OW, F16), "pl": _sb(NB, U16),
+    "orow": _sb(C, F32), "oext": _sb(C, F32), "ol": _sb(NB, U16), "ysb": _sb(C, F32),
+    "rt": _sb(NB, F32),
+}
+for _t in range(4):
+    SCRATCH["xc%d" % _t] = _sb(C, Q4)
+    SCRATCH["xs%d" % _t] = _sb(C, U8)
+for _t in range(3):
+    SCRATCH["lc%d" % _t] = _sb(C, Q4)
+    SCRATCH["ls%d" % _t] = _sb(C, U8)
+    SCRATCH["rc%d" % _t] = _sb(C, Q4)
+    SCRATCH["rs%d" % _t] = _sb(C, U8)
+    SCRATCH["lm%d" % _t] = _sb(LM0 + NB + 2, F32)
+    SCRATCH["tl%d" % _t] = _sb(NB, F32)
+
+LABELS = """ldx ldu ldw ldv gi0 gi1 gi2 gi3 ge ge2 fill ul q0 q1 q2 q3 q4 qs hot keep kz mx mo taba w0 qu pc ps qx qxh sh sa sb s1 sm hs smh hsh
+cmp sg acc cs lm wt cum e1 e2 take n1 n2 n16 name p1 p2 p3 qe qv ca cb cs2 mm m16 a32 al ad bd dout a16 b16 v1 v2 scan pl pl7 orow oext ol
+d0 d1 d2 d3 dev zv zs qz z3v z3s r0 r1 r2 r3 add0 add1 add2 add3 xs xv ym ym1 yc yc1 sto sts""".split()
+SEMAPHORES = LABELS + ["out"] + ["%s%d" % (n, t) for n in ("bulk", "tab", "hc", "hsc", "ht") for t in range(3)]
+
+
+def _helpers(topo, T, r):
+    c = T.cores[r]
+    return [h for h in topo.cores_of(c) if T.rank_of(h) is None and topo.die(h) == topo.die(c)
+            and all(topo.may_write(h, T.cores[r ^ m]) for m in MASKS)][:2]
+
+
+def _mask(engines):
+    return sum(1 << e for e in engines)
+
+
+def _write(g, T, topo, src, dst, out, in_, sem):
+    rid, pid = topo.addr(dst, src)
+    g.remote_dma(out, in_, T.sem[sem], T.sem.out, pid, rid, topo.mask(src, dst))
+    return len(topo.engines(src, dst))
+
+
+def _helper_program(g, core, T, topo, r, i):
+    own, sent = T.cores[r], 0
+    n = len(topo.engines(own, core))
+    for t, m in enumerate(MASKS):
+        far = T.cores[r ^ m]
+        near, hop = far in topo.cores_of(own), not topo.may_write(own, far)
+        half = not (near or hop)
+        a, b = (H * i, H * i + H) if half else (0, C)
+        if half or (hop and i == 1):
+            g.wait_ge(T.sem["hc%d" % t], n // 2 if half else n)
+            sent += _write(g, T, topo, core, far, T["lc%d" % t][:, a:b].bitcast(dt.uint8), T["rc%d" % t][:, 0:b - a].bitcast(dt.uint8), "bulk%d" % t)
+        if half or i == 0:
+            g.wait_ge(T.sem["hsc%d" % t], n // 2 if half else n)
+            sent += _write(g, T, topo, core, far, T["ls%d" % t][:, a:b], T["rs%d" % t][:, 0:b - a], "bulk%d" % t)
+        if hop and i == 0:
+            g.wait_ge(T.sem["ht%d" % t], n)
+            sent += _write(g, T, topo, core, far, T["tl%d" % t][:], T.rt[:], "tab%d" % t)
+    g.wait_ge(T.sem.out, sent)
+
+
+def _emit(g, T, ops):
+    queue = {"g": g, "v": g.vector, "s": g.scalar, "t": g.tensor, "y": g.sync}
+    know = {k: 0 for k in queue}
+    count, members, waited = {}, {}, {}
+    writer, readers = {}, {}
+    for n, o in enumerate(ops):
+        q, need = o["q"], set()
+        for k in o["r"] + o["w"]:
+            if k in writer:
+                need.add(writer[k])
+        for k in o["w"]:
+            need.update(readers.get(k, []))
+        for d in sorted(need, reverse=True):
+            if know[q] >> d & 1:
+                continue
+            lab = ops[d]["label"]
+            queue[q].wait_ge(T.sem[lab], count[lab])
+            waited[lab] = count[lab]
+            for e in members[lab]:
+                know[q] |= ops[e]["know"] | 1 << e
+        for s, v in o["ext"]:
+            queue[q].wait_ge(T.sem[s], v)
+        o["know"] = know[q]
+        ins = o["fn"](queue[q])
+        if o["label"] is None:
+            continue
+        ins.then_inc(T.sem[o["label"]], o["inc"])
+        count[o["label"]] = count.get(o["label"], 0) + o["inc"]
+        members.setdefault(o["label"], []).append(n)
+        for k in o["r"]:
+            readers.setdefault(k, []).append(n)
+        for k in o["w"]:
+            writer[k], readers[k] = n, []
+    for lab in count:
+        if waited.get(lab, 0) < count[lab]:
+            g.wait_ge(T.sem[lab], count[lab])
+
+
+def rank_program(g, core, T, topo):
+    rank = T.rank_of(core)
+    if rank is None:
+        for r in range(len(T.cores)):
+            hs = _helpers(topo, T, r)
+            if core in hs:
+                _helper_program(g, core, T, topo, r, hs.index(core))
+        return
+    A, F = AluOpType, ActivationFunctionType
+    ops, sent = [], [0]
+    helpers = _helpers(topo, T, rank)
+
+    def op(q, label, fn, r="", w="", ext=(), inc=1):
+        ops.append({"q": q, "label": label, "fn": fn, "r": r.split(), "w": w.split(), "ext": list(ext), "inc": inc})
+
+    def ts(label, out, in0, s1, o0, s2=None, o1=None, r="", w=""):
+        if o1 is None:
+            op("v", label, lambda e: e.tensor_scalar(out, in0, s1, None, o0), r, w)
+        else:
+            op("v", label, lambda e: e.tensor_scalar(out, in0, s1, s2, o0, o1), r, w)
+
+    def tt(label, out, a, b, o, r="", w="", ext=()):
+        op("v", label, lambda e: e.tensor_tensor(out, a, b, o), r, w, ext)
+
+    def cp(label, out, a, r="", w=""):
+        op("v", label, lambda e: e.tensor_copy(out, a), r, w)
+
+    def scan(label, out, a, b, init, o0, o1, r="", w=""):
+        op("v", label, lambda e: e.tensor_tensor_scan(out, a, b, init, o0, o1), r, w)
+
+    def fill(label, ap, c, w):
+        op("v", label, lambda e: e.memset(ap, c), "", w)
+
+    def act(label, out, a, f, r="", w="", **kw):
+        op("s", label, lambda e: e.activation(out, a, f, **kw), r, w)
+
+    def lin(label, out, a, scale, bias, r, w):
+        act(label, out, a, F.Identity, r, w, scale=scale, bias=bias)
+
+    def quant(label, c, s, a, r, w):
+        op("v", label, lambda e: e.quantize_mx(c, s, a), r, w)
+
+    def mm(label, b, lc, ls, rc, rs, r, ext=(), n=C):
+        op("t", label, lambda e: e.matmul_mx(bank(b, n), lc, ls, rc, rs, True, True), r, "ps%d" % b, ext)
+
+    def dma(q, label, out, a, r="", w=""):
+        op(q, label, lambda e: e.dma_start(out, a), r, w, inc=16)
+
+    def iota(label, out, pattern, base, cm, w, small=True):
+        if small:
+            op("g", label, lambda e: e.iota(out, pattern, base, cm, allow_small_or_imprecise_dtypes=True), "", w)
+        else:
+            op("g", label, lambda e: e.iota(out, pattern, base, cm), "", w)
+
+    def bank(b, n=C):
+        return T.ps[:, 512 * b:512 * b + n]
+
+    def col(j):
+        return T.cc[:, j:j + 1]
+
+    def write(dst, out, a, sem, r):
+        def fn(e):
+            sent[0] += _write(e, T, topo, core, dst, out, a, sem)
+        op("g", None, fn, r)
+
+    def halves(outs, ins, sem, r):
+        def fn(e):
+            xs = []
+            for i, h in enumerate(helpers):
+                rid, pid = topo.addr(h, core)
+                en = topo.engines(core, h)
+                en = en[len(en) // 2 * i:len(en) // 2 * (i + 1)]
+                xs.append(RemoteDMATransfer(dst_ids=[DstId(rid=rid, pnc=pid)], dma_engine_mask=_mask(en), remote_sem=T.sem[sem], src=ins[i], dst=outs))
+                sent[0] += len(en)
+            e.remote_dma_fused(xs, local_sem=T.sem.out)
+        op("g", None, fn, r)
+
+    u8 = dt.uint8
+
+    dma("y", "ldx", T.xt[:], T.x[:], w="x0 x1 x2 x3")
+    dma("s", "ldu", T.ut[:], T.u[:], w="ut")
+    iota("gi0", T.uli[:], [[1, 2], [16, 8]], 0, 0, "uli", small=False)
+    iota("gi0", T.pi[:, 0:1], [[1, 1]], 0, 1, "pi0", small=False)
+    iota("gi1", T.tmp[:], [[0, NB], [8, 16]], 4, 0, "tmp")
+    iota("gi2", T.iot[:], [[1, 2 * C]], 0, 0, "iot")
+    iota("gi3", T.tmn[:], [[0, NB], [-8, 16]], 4, 0, "tmn")
+    fill("fill", T.keep[:, 0:SEG], 1.0, "keep")
+    ts("q0", T.pi[:, 1:2], T.pi[:, 0:1], 15, A.bitwise_and, r="pi0", w="pi1")
+    cp("ul", T.ul[:], T.uli[:], "uli", "ul")
+    cp("q1", col(0), T.pi[:, 1:2], "pi1", "c0")
+    fill("q4", T.cap[:], float(CAP), "cap")
+    ts("q2", col(1), col(0), 8.0, A.mult, r="c0", w="c1")
+    ts("q2", col(2), col(0), float(1 - JUNK), A.add, 1.0, A.max, "c0", "c2")
+    ts("q2", col(4), col(0), 15.0, A.is_equal, r="c0", w="c4")
+    ts("keep", T.keepf[:], T.tmp[:, 0:LO], col(1), A.subtract, 4.0, A.not_equal, "tmp c1", "keepf")
+    ts("hot", T.hot[:], T.tmp[:], col(1), A.subtract, 4.0, A.is_equal, "tmp c1", "hot")
+    ts("q3", col(3), col(2), 1.0, A.add, col(2), A.mult, "c2", "c3")
+    ts("q4", col(5), T.pi[:, 0:1], -4.0, A.mult, -2.0, A.add, "pi0", "c5")
+    fill("q4", T.cum[:, 0:1], 0.0, "cum0")
+    fill("q4", T.a16[:, C:C + 1], -TOP, "a16e")
+    fill("q4", T.b16[:, C:C + 1], 0.0, "b16e")
+    ts("q4", T.lists[:, 0:1], col(3), 8.0, A.mult, -1.0, A.add, "c3", "ends")
+    ts("mx", T.mx[:], T.hot[:], -8320.0, A.mult, 128.0, A.add, "hot", "mx")
+    act("kz", T.keep[:, SEG:SEG + HI], T.keepf[:, HI - 1::-1], F.Copy, "keepf", "keepr")
+    for k in range(KV):
+        act("kz", T.keep[:, 8 * k * (k + 1):8 * k * (k + 1) + 16], T.keepf[:, 15::-1], F.Copy, "keepf keep", "keep%d" % k)
+    lin("qs", col(7), col(4), 4.0, -WIPE - 4.0, "c4", "c7")
+    lin("qs", col(8), col(4), -1.0, 1.0, "c4", "c8")
+    lin("qs", col(9), col(0), 1024.0, -15360.0, "c0", "c9")
+    lin("qs", T.ad[:, 0:1], col(4), 0.0, WIPE, "c4", "ad0")
+    lin("qs", T.bd[:, 0:1], col(4), 4.0, -WIPE - 4.0, "c4", "bd0")
+    quant("qu", T.uc[:], T.us[:], T.ut[:], "ut", "uq")
+    cp("pc", T.upc[:].bitcast(dt.uint32), T.uc[:].bitcast(dt.uint32).indirect(T.ul[:]), "uq ul", "upc")
+    act("ps", T.ups[:], T.us[:].indirect(T.ul[:]), F.Copy, "uq ul", "ups")
+    act("ge", T.dist[:], T.iot[:, 0:518], F.Abs, "iot c5", "dist", bias=col(5))
+    ts("cb", T.cb[:], T.tmp[:], col(1), A.subtract, -4.0, A.max, "tmp c1", "cb")
+
+    def send_state(t):
+        far = T.cores[rank ^ MASKS[t]]
+        xc, xs, key = T["xc%d" % t], T["xs%d" % t], "xq%d xq%dh" % (t, t)
+        theirs = [len(topo.engines(h, core)) for h in _helpers(topo, T, rank ^ MASKS[t])]
+        if far in topo.cores_of(core):
+            write(helpers[0], T["rs%d" % t][:], xs[:], "hsc%d" % t, key)
+            write(far, T["lc%d" % t][:].bitcast(u8), xc[:].bitcast(u8), "bulk%d" % t, key)
+            return len(topo.engines(far, core)) + theirs[0]
+        if not topo.may_write(core, far):
+            write(helpers[0], T["rs%d" % t][:], xs[:], "hsc%d" % t, key)
+            write(helpers[1], T["rc%d" % t][:].bitcast(u8), xc[:].bitcast(u8), "hc%d" % t, key)
+            return sum(theirs)
+        halves(T["rc%d" % t][:, 0:H].bitcast(u8), [xc[:, H * i:H * i + H].bitcast(u8) for i in range(2)], "hc%d" % t, key)
+        halves(T["rs%d" % t][:, 0:H], [xs[:, H * i:H * i + H] for i in range(2)], "hsc%d" % t, key)
+        return 2 * sum(theirs)
+
+    def send_table(t):
+        far = T.cores[rank ^ MASKS[t]]
+        lm = T["lm%d" % t][:, LM0:LM0 + NB]
+        if topo.may_write(core, far):
+            write(far, T["tl%d" % t][:], lm, "tab%d" % t, "lma%d lmb%d" % (t, t))
+            return len(topo.engines(far, core))
+        write(helpers[0], T.rt[:], lm, "ht%d" % t, "lma%d lmb%d" % (t, t))
+        return len(topo.engines(_helpers(topo, T, rank ^ MASKS[t])[0], core))
+
+    def own(b):
+        return T.win[:, 2 * C * b:2 * C * b + C]
+
+    for t in range(3):
+        xc, xs, xq = T["xc%d" % t], T["xs%d" % t], "xq%d" % t
+        lmb = T["lm%d" % t]
+        lm, lmk = lmb[:, LM0:LM0 + NB], "lma%d lmb%d" % (t, t)
+        quant("qxh", xc[:, CUT:C], xs[:, CUT:C], T.xt[:, 4 * CUT:4 * C], "x0 x1 x2 x3", xq + "h")
+        quant("qx", xc[:, 0:CUT], xs[:, 0:CUT], T.xt[:, 0:4 * CUT], "x0 x1 x2 x3", xq)
+        mm("sh", 7, T.upc[:, 0:128], T.ups[:, 0:128], xc[:, CUT:C], xs[:, CUT:C], "upc ups %sh" % xq, n=128)
+        xq += " %sh" % xq
+        nbulk = send_state(t)
+        mm("sa", 0, T.upc[:, 0:128], T.ups[:, 0:128], xc[:, 0:LO], xs[:, 0:LO], "upc ups " + xq, n=LO)
+        mm("sb", 1, T.upc[:, 0:128], T.ups[:, 0:128], xc[:], xs[:], "upc ups " + xq)
+        mm("s1", 2, T.upc[:, 128:256], T.ups[:, 128:256], xc[:], xs[:], "upc ups " + xq)
+        if t == 0:
+            dma("y", "ldw", T.wq[:].bitcast(u8), T.wc[:], "x0", "wq")
+            dma("y", "ldw", T.wp[:], T.ws[:], "", "wp")
+            dma("y", "ldv", T.vt[:], T.v[:], "", "vt")
+        back = T.ps[:, 512 * 7 + 127:512 * 7 + 127 - HI:-1]
+        tt("smh", T.sm[:, LO:C], back, T.hot[:, HI - 1::-1], A.mult, "ps7 hot", "smh")
+        scan("hsh", T.hs[:, LO:C], T.keep[:, SEG:SEG + HI], T.sm[:, LO:C], 0.0, A.mult, A.add, "keepr smh", "hsh")
+        tt("sm", T.sm[:, 0:LO], bank(0, LO), T.hot[:, 0:LO], A.mult, "ps0 hot", "sm")
+        tt("cmp", T.cmp[:, SEG:SEG + HI], back, T.hs[:, LO:C], A.is_ge, "ps7 hsh", "cmpd")
+        scan("hs", T.hs[:, 0:LO], T.keepf[:], T.sm[:, 0:LO], 0.0, A.mult, A.add, "keepf sm", "hs")
+        for k in range(KV):
+            n = 16 * (k + 1)
+            ts("cmp", T.cmp[:, 8 * k * (k + 1):8 * k * (k + 1) + n], T.ps[:, n - 1::-1], T.hs[:, n - 1:n], A.is_ge, r="ps0 hs", w="cmp%d" % k)
+        for k in range(KV, NB):
+            n, a, c = 16 * k, C * (k - KV), LO + 16 * (NB - k) - 1
+            act("sg", T.sg[:, a:a + n], bank(1, n), F.Sign, "ps1 hsh", "sg%d" % k, scale=-1.0, bias=T.hs[:, c:c + 1])
+        for k in range(KV, NB):
+            n, a = 16 * k, C * (k - KV)
+            act("acc", T.sr[:, a:a + n], T.sg[:, a:a + n], F.Sign, "sg%d" % k, "acc%d" % k, scale=-1.0, bias=1.0,
+                accum_out=T.acc[:, k - KV:k - KV + 1])
+        scan("cs", T.cs[:], T.keep[:], T.cmp[:], 0.0, A.mult, A.add, "keep keepr cmpd " + " ".join("cmp%d keep%d" % (k, k) for k in range(KV)), "cs")
+        cp("lm", lmb[:, LM0 - JUNK:LM0 + KV], T.cs[:, 0:SEG].indirect(T.lists[:, 0:1]), "cs ends", "lma%d" % t)
+        tt("lm", lmb[:, LM0 + KV:LM0 + NB], T.acc[:], T.cs[:, SEG + HI - 1:SEG:-16], A.add,
+           "cs " + " ".join("acc%d" % k for k in range(KV, NB)), "lmb%d" % t)
+        ntab = send_table(t)
+        if t == 0:
+            ts("ca", T.ca[:], T.tmn[:], col(1), A.add, 4.0, A.min, "tmn c1", "ca")
+            act("ge2", T.eb[:, 0:516], T.dist[:, 0:516], F.Relu, "dist", "eb", scale=-1.0, bias=1.0)
+            act("ge2", T.eb[:, 517:1032], T.dist[:, 0:515], F.Relu, "dist", "eb2", scale=-1.0, bias=1.0)
+            lin("cs2", T.eb[:, 516:517], col(4), 0.0, 0.0, "c4", "eb3")
+            lin("cs2", T.iod[:], T.iot[:, 0:C:16], 1.0, col(0), "iot c0", "iod")
+            lin("cs2", T.ca[:, 15:C:16], T.iot[:, 0:NB], 0.0, WIPE, "iot", "ca")
+            lin("cs2", T.cb[:, 15:C:16], T.iot[:, 0:NB], 0.0, col(7), "iot c7", "cb")
+            for a in (0, C):
+                b = min(a, 1)
+                lin("taba", T.taba[:, a + b:a + C + 1], T.iot[:, b:C + 1], -2 * U, 291.25 * U, "iot", "taba%d" % a)
+                lin("taba", T.tabb[:, a + b:a + C + 1], T.iot[:, b:C + 1], 2 * U, -290.5 * U, "iot", "tabb%d" % a)
+        ts("wt", T.wt[:], bank(2), 0.0, A.is_gt, r="ps2", w="wt")
+        ts("p2", T.p2[:], lm, float(C), A.add, r=lmk, w="p2")
+        scan("cum", T.cum[:, 1:C + 1], T.wt[:], T.cap[:], 0.0, A.add, A.min, "wt cap", "cum")
+        scan("e1", T.e1[:], T.mx[:], T.cum[:, 1:C + 1], 0.0, A.add, A.max, "mx cum", "e1")
+        scan("e2", T.e2[:], T.mx[:], T.cum[:, 0:C], 0.0, A.add, A.max, "mx cum cum0", "e2")
+        tt("take", T.take[:], T.e1[:, 15:C:16], T.e2[:, 15:C:16], A.subtract, "e1 e2", "take")
+        tt("p1", T.p1[:], T.p2[:], T.take[:], A.mult, "take p2", "p1")
+        ts("n1", T.n1[:], T.take[:], float(C), A.mult, r="take", w="n1")
+        tt("p3", T.p3[:], T.p2[:], T.p1[:], A.subtract, "p1 p2", "p3")
+        tt("n2", T.n2[:], T.n1[:], T.iod[:], A.add, "n1 iod", "n2")
+        if t == 0:
+            for b in range(4):
+                a = 516 * (b % 2) + 2 - b // 2 * 2
+                quant("qe", T.ec[:, 128 * b:128 * b + 128], T.es[:, 128 * b:128 * b + 128], T.eb[:, a:a + 512], "eb eb2 eb3", "eq%d" % b)
+        if t == 1:
+            quant("qv", T.vc[:], T.vs[:], T.vt[:], "vt", "vq")
+        cp("n16", T.n16[:], T.n2[:], "n2", "n16")
+        tt("mm", T.mm[:], T["tl%d" % t][:], T.p3[:], A.max, "p3", "mm", ext=[("tab%d" % t, ntab)])
+        cp("m16", T.m16[:], T.mm[:], "mm", "m16")
+        act("a32", T.a32[:], T.taba[:].indirect(T.m16[:]), F.Copy, "taba0 taba288 m16", "a32")
+        op("g", "a16", lambda e: e.affine_select(T.a16[:, 0:C], T.a32[:], [[0, C]], A.is_gt, 0.0, 1, 0), "a32", "a16")
+        lin("al", T.al[:], T.a32[:, 15:C:16], col(8), 0.0, "a32 c8", "al")
+        lin("al", T.bl[:], T.a32[:, 15:C:16], -1.0, 0.75 * U, "a32", "bl")
+        act("name", T.name[:], T.iot[:].indirect(T.n16[:]), F.Copy, "iot n16", "name")
+        if t == 0:
+            lin("mo", T.mo[:], T.hot[:], -66560.0, 1024.0, "hot", "mo")
+            for b in range(4):
+                act("w0", own(b), T.xt[:, b:4 * C:4], F.Copy, "x%d" % b, "own%d" % b, scale=32.0)
+        tt("ad", T.ad[:, 1:C + 1], T.taba[:].indirect(T.m16[:]), T.ca[:], A.max, "taba0 taba288 m16 ca", "ad")
+        tt("bd", T.bd[:, 1:C + 1], T.tabb[:].indirect(T.m16[:]), T.cb[:], A.min, "tabb0 tabb288 m16 cb", "bd")
+        scan("dout", T.dout[:], T.ad[:, 0:C], T.bd[:, 0:C], TOP, A.add, A.add, "ad bd ad0 bd0", "dout")
+        tt("v1", T.v1[:], T.dout[:, 15:C:16], T.al[:], A.add, "dout al", "v1")
+        ts("b16", T.b16[:, 0:C], T.a16[:, 0:C], -1.0, A.mult, 0.75 * U, A.add, "a16", "b16")
+        tt("v2", T.v2[:], T.v1[:], T.bl[:], A.add, "v1 bl", "v2")
+        for k in range(NB - 1):
+            a = 16 * k + 16
+            scan("scan", T.o16[:, OW * k + 16 * k:OW * k + OW], T.a16[:, a:C + 1], T.b16[:, a:C + 1], T.v2[:, k:k + 1], A.add, A.add,
+                 "a16 b16 a16e b16e v2", "o%d" % k)
+        ts("pl7", T.pl[:, NB - 1:NB], T.v2[:, NB - 1:NB], 0.5 / U, A.mult, H - TOP * 0.5 / U, A.add, "v2", "pl7")
+        ts("pl", T.pl[:, 0:NB - 1], T.o16[:, OW - 1:OW * (NB - 1):OW], 0.5 / U, A.mult, float(H), A.add, " ".join("o%d" % k for k in range(NB - 1)), "pl")
+        for b in range(4):
+            mm("d%d" % b, 3 + b, T.ec[:, 128 * b:128 * b + 128], T.es[:, 128 * b:128 * b + 128], T["lc%d" % t][:], T["ls%d" % t][:],
+               "eq%d" % b, ext=[("bulk%d" % t, nbulk)] if b == 0 else [])
+        for b in range(4):
+            act("dev", T.win[:, 2 * C * b + C:2 * C * b + 2 * C], bank(3 + b), F.Copy, "ps%d" % (3 + b), "far%d" % b, scale=32.0)
+        cp("orow", T.orow[:].indirect(T.pl[:]), T.name[:], "pl pl7 name", "orow")
+        scan("oext", T.oext[:], T.mo[:], T.orow[:], 0.0, A.add, A.max, "mo orow", "oext")
+        ts("ol", T.ol[:], T.oext[:, 15:C:16], col(9), A.add, r="oext c9", w="ol")
+        if t == 2:
+            dma("y", "sto", T.od[:], T.orow[0:128:16, :], "orow")
+        for b in range(4):
+            src, key = T.win[:, 2 * C * b:2 * C * b + 2 * C].indirect(T.ol[:]), "own%d far%d ol" % (b, b)
+            if b < 2:
+                ts("zv", T.zt[:, b:4 * C:4], src, 0.03125, A.mult, r=key, w="z%d" % b)
+            else:
+                act("zs", T.zt[:, b:4 * C:4], src, F.Copy, key, "z%d" % b, scale=0.03125)
+        quant("qz", T.zc[:], T.zs[:], T.zt[:], "z0 z1 z2 z3", "zq")
+        for b in range(4):
+            if b < 2:
+                ts("z3v", T.z32[:, C * b:C * b + C], T.zt[:, b:4 * C:4], 32.0, A.mult, r="z%d" % b, w="y%d" % b)
+            else:
+                act("z3s", T.z32[:, C * b:C * b + C], T.zt[:, b:4 * C:4], F.Copy, "z%d" % b, "y%d" % b, scale=32.0)
+        for b in range(4):
+            mm("r%d" % b, 3 + b, T.wq[:, 128 * b:128 * b + 128], T.wp[:, 128 * b:128 * b + 128], T.zc[:], T.zs[:], "wq wp zq")
+        for b in range(4):
+            tt("add%d" % b, own(b), bank(3 + b), T.z32[:, C * b:C * b + C], A.add, "ps%d y%d" % (3 + b, b), "own%d" % b)
+        for b in range(3):
+            act("xs", T.xt[:, b:4 * C:4], own(b), F.Copy, "own%d" % b, "x%d" % b, scale=0.03125)
+        ts("xv", T.xt[:, 3:4 * C:4], own(3), 0.03125, A.mult, r="own3", w="x3")
+
+    quant("qxh", T.xc3[:, 0:H], T.xs3[:, 0:H], T.xt[:, 0:4 * H], "x0 x1 x2 x3", "xq3h")
+    quant("qx", T.xc3[:, H:C], T.xs3[:, H:C], T.xt[:, 4 * H:4 * C], "x0 x1 x2 x3", "xq3")
+    mm("ym", 0, T.vc[:], T.vs[:], T.xc3[:, 0:H], T.xs3[:, 0:H], "vq xq3h", n=H)
+    mm("ym1", 1, T.vc[:], T.vs[:], T.xc3[:, H:C], T.xs3[:, H:C], "vq xq3", n=H)
+    cp("yc", T.ysb[:, 0:H], bank(0, H), "ps0", "ysb")
+    act("yc1", T.ysb[:, H:C], bank(1, H), F.Copy, "ps1", "ysb1")
+    dma("y", "sto", T.oc[:], T.xc3[:].bitcast(u8), "xq3 xq3h")
+    dma("y", "sto", T.y[:], T.ysb[:], "ysb ysb1")
+    for k in range(4):
+        dma("s", "sts", T.osc[4 * k:4 * k + 4, :], T.xs3[32 * k:32 * k + 4, :], "xq3 xq3h")
+    _emit(g, T, ops)
+    g.wait_ge(T.sem.out, sent[0])

@@ -1,19 +1,28 @@
-from concourse.bass import DstId, RemoteDMATransfer
 from concourse.mybir import dt, AluOpType, ActivationFunctionType
 
 C, CAP, NB = 288, 128, 18
 MASKS = [1, 2, 4]
-KV = 13
-SEG = 8 * KV * (KV + 1)
-JUNK = 16 - KV
-LO, HI = 16 * KV, C - 16 * KV
-CUT = C - 128
-LM0 = 4
-H = C // 2
+KV = 8
+LO = 16 * KV
+HALF = {"h": (LO, C), "l": (0, LO)}
+PAIRS = {"l": (0, KV // 2, 16 * (KV + 1) + 4, 0), "h": (KV, (NB - KV) // 2, 16 * (NB + KV + 1) + 4, (16 * (KV + 1) + 4) * KV // 2)}
+TOT = PAIRS["h"][3] + PAIRS["h"][1] * PAIRS["h"][2]
+LAYER = ("gh0v gh2s gh1v gh3s gl0v gl2s gl3s gl1s qh zhv ql zls ah0 xh0s ah1 xh1s ah2 xh2s ah3 xh3s "
+         "al0 al1 al2 al3 xl0s xl1s xl2s Qh xl3v Ql mh").split()
 U = 2.0 ** -10
 TOP = 2.0 ** 14
-WIPE = 2.0 ** 25
+WIPE = 1.5 * 2.0 ** 23
+BASE = 2.0 ** 23
+PARK = 2.0 ** 40
+SHIFT = 64.0
 OW = C - 16 + 1
+
+
+def _start(k):
+    k0, n, w, p = PAIRS["l" if k < KV else "h"]
+    j = k - k0
+    return p + (w * j if j < n else (w + 16) * (2 * n - 1 - j) + 16 * k0 + 18)
+
 
 F32, BF, F16, U16, I32, Q4, U8 = "float32", "bfloat16", "float16", "uint16", "int32", "float8_e4m3fn_x4", "uint8"
 
@@ -25,22 +34,21 @@ def _sb(n, t):
 SCRATCH = {
     "ps": ("psum", [128, 4096], F32),
     "xt": _sb(4 * C, BF), "ut": _sb(512, BF), "vt": _sb(512, BF), "zt": _sb(4 * C, BF), "z32": _sb(4 * C, BF),
-    "win": _sb(8 * C, BF),
+    "win0": _sb(8 * C, BF), "win1": _sb(8 * C, BF),
     "uc": _sb(128, Q4), "us": _sb(128, U8), "upc": _sb(256, Q4), "ups": _sb(256, U8),
     "vc": _sb(128, Q4), "vs": _sb(128, U8), "ec": _sb(512, Q4), "es": _sb(512, U8),
     "wq": _sb(512, Q4), "wp": _sb(512, U8), "zc": _sb(C, Q4), "zs": _sb(C, U8),
-    "dist": _sb(518, BF), "eb": _sb(1032, BF),
-    "uli": _sb(16, I32), "ul": _sb(16, U16), "pi": _sb(2, I32), "cc": _sb(16, F32), "lists": _sb(4, U16),
-    "iot": _sb(2 * C, F32), "tmp": _sb(C, F32), "tmn": _sb(C, F32), "hot": _sb(C, BF), "keep": _sb(SEG + HI, BF), "keepf": _sb(LO, BF),
-    "mx": _sb(C, F16), "mo": _sb(C, F32), "cap": _sb(C, F16), "iod": _sb(NB, F32),
-    "taba": _sb(2 * C + 1, F32), "tabb": _sb(2 * C + 1, F32), "ca": _sb(C, F32), "cb": _sb(C, F32),
-    "sm": _sb(C, F32), "hs": _sb(C, F32), "cmp": _sb(SEG + HI, BF), "cs": _sb(SEG + HI, BF),
-    "sg": _sb((NB - KV) * C, BF), "sr": _sb((NB - KV) * C, BF), "acc": _sb(NB - KV, F32),
+    "one": _sb(516, BF), "eb": _sb(1032, BF),
+    "uli": _sb(16, I32), "ul": _sb(16, U16), "pi": _sb(2, I32), "cc": _sb(16, F32),
+    "iot": _sb(2 * C, F32), "tmp": _sb(C, BF), "hot": _sb(C, BF), "hop": _sb(LO, BF), "keep": _sb(C - LO, BF),
+    "mx": _sb(C, BF), "mo": _sb(C, F32), "cap": _sb(C, BF), "iod": _sb(NB, F32),
+    "taba": _sb(2 * C, F32), "tabb": _sb(2 * C, F32), "ca": _sb(C, BF), "cb": _sb(C, F32),
+    "sm": _sb(C, F32), "hs": _sb(C, F32), "cmp": _sb(TOT, BF), "cs": _sb(TOT, BF), "dl": _sb(TOT, BF), "pat": _sb(18, BF),
     "wt": _sb(C, F16), "cum": _sb(C + 2, F16), "e1": _sb(C, F16), "e2": _sb(C, F16),
-    "take": _sb(NB, F32), "n1": _sb(NB, F32), "n2": _sb(NB, F32), "n16": _sb(NB, U16), "name": _sb(C, F32),
-    "p1": _sb(NB, F32), "p2": _sb(NB, F32), "p3": _sb(NB, F32),
+    "own": _sb(NB, F32), "n1": _sb(NB, F32), "n2": _sb(NB, F32), "n16": _sb(NB, U16), "name": _sb(C, F32),
+    "p2": _sb(NB, F32), "p3": _sb(NB, F32),
     "mm": _sb(NB, F32), "m16": _sb(NB, U16),
-    "a32": _sb(C, F32), "ad": _sb(C + 1, F32), "bd": _sb(C + 1, F32), "dout": _sb(C, F32),
+    "a32": _sb(C, F32), "ad": _sb(C, F32), "bd": _sb(C, F32), "dout": _sb(C, F32),
     "al": _sb(NB, F32), "bl": _sb(NB, F32), "v1": _sb(NB, F32), "v2": _sb(NB, F32),
     "a16": _sb(C + 2, F16), "b16": _sb(C + 2, F16), "o16": _sb((NB - 1) * OW, F16), "pl": _sb(NB, U16),
     "orow": _sb(C, F32), "oext": _sb(C, F32), "ol": _sb(NB, U16), "ysb": _sb(C, F32),
@@ -54,23 +62,17 @@ for _t in range(3):
     SCRATCH["ls%d" % _t] = _sb(C, U8)
     SCRATCH["rc%d" % _t] = _sb(C, Q4)
     SCRATCH["rs%d" % _t] = _sb(C, U8)
-    SCRATCH["lm%d" % _t] = _sb(LM0 + NB + 2, F32)
+    SCRATCH["lm%d" % _t] = _sb(NB + 2, F32)
     SCRATCH["tl%d" % _t] = _sb(NB, F32)
 
-LABELS = """ldx ldu ldw ldv gi0 gi1 gi2 gi3 ge ge2 fill ul q0 q1 q2 q3 q4 qs hot keep kz mx mo taba w0 qu pc ps qx qxh sh sa sb s1 sm hs smh hsh
-cmp sg acc cs lm wt cum e1 e2 take n1 n2 n16 name p1 p2 p3 qe qv ca cb cs2 mm m16 a32 al ad bd dout a16 b16 v1 v2 scan pl pl7 orow oext ol
-d0 d1 d2 d3 dev zv zs qz z3v z3s r0 r1 r2 r3 add0 add1 add2 add3 xs xv ym ym1 yc yc1 sto sts""".split()
-SEMAPHORES = LABELS + ["out"] + ["%s%d" % (n, t) for n in ("bulk", "tab", "hc", "hsc", "ht") for t in range(3)]
+LOCAL = ["s%d" % _t for _t in range(130)]
+SEMAPHORES = LOCAL + ["out"] + ["%s%d" % (n, t) for n in ("bulk", "tab", "hc", "hd", "hsc", "ht") for t in range(3)]
 
 
 def _helpers(topo, T, r):
     c = T.cores[r]
     return [h for h in topo.cores_of(c) if T.rank_of(h) is None and topo.die(h) == topo.die(c)
             and all(topo.may_write(h, T.cores[r ^ m]) for m in MASKS)][:2]
-
-
-def _mask(engines):
-    return sum(1 << e for e in engines)
 
 
 def _write(g, T, topo, src, dst, out, in_, sem):
@@ -82,27 +84,29 @@ def _write(g, T, topo, src, dst, out, in_, sem):
 def _helper_program(g, core, T, topo, r, i):
     own, sent = T.cores[r], 0
     n = len(topo.engines(own, core))
+    u8 = dt.uint8
     for t, m in enumerate(MASKS):
         far = T.cores[r ^ m]
         near, hop = far in topo.cores_of(own), not topo.may_write(own, far)
-        half = not (near or hop)
-        a, b = (H * i, H * i + H) if half else (0, C)
-        if half or (hop and i == 1):
-            g.wait_ge(T.sem["hc%d" % t], n // 2 if half else n)
-            sent += _write(g, T, topo, core, far, T["lc%d" % t][:, a:b].bitcast(dt.uint8), T["rc%d" % t][:, 0:b - a].bitcast(dt.uint8), "bulk%d" % t)
-        if half or i == 0:
-            g.wait_ge(T.sem["hsc%d" % t], n // 2 if half else n)
-            sent += _write(g, T, topo, core, far, T["ls%d" % t][:, a:b], T["rs%d" % t][:, 0:b - a], "bulk%d" % t)
-        if hop and i == 0:
+        lc, rc = T["lc%d" % t], T["rc%d" % t]
+        if i == 0 and (near or hop):
+            g.wait_ge(T.sem["hsc%d" % t], n)
+            sent += _write(g, T, topo, core, far, T["ls%d" % t][:], T["rs%d" % t][:], "bulk%d" % t)
+        if i == 0 and hop:
             g.wait_ge(T.sem["ht%d" % t], n)
             sent += _write(g, T, topo, core, far, T["tl%d" % t][:], T.rt[:], "tab%d" % t)
+            g.wait_ge(T.sem["hd%d" % t], n)
+            sent += _write(g, T, topo, core, far, lc[:, 0:LO].bitcast(u8), rc[:, 0:LO].bitcast(u8), "bulk%d" % t)
+        if i == 1 and hop:
+            g.wait_ge(T.sem["hc%d" % t], n)
+            sent += _write(g, T, topo, core, far, lc[:, LO:C].bitcast(u8), rc[:, LO:C].bitcast(u8), "bulk%d" % t)
     g.wait_ge(T.sem.out, sent)
 
 
 def _emit(g, T, ops):
     queue = {"g": g, "v": g.vector, "s": g.scalar, "t": g.tensor, "y": g.sync}
     know = {k: 0 for k in queue}
-    count, members, waited = {}, {}, {}
+    sem, count, members, waited = {}, {}, {}, {}
     writer, readers = {}, {}
     for n, o in enumerate(ops):
         q, need = o["q"], set()
@@ -115,7 +119,7 @@ def _emit(g, T, ops):
             if know[q] >> d & 1:
                 continue
             lab = ops[d]["label"]
-            queue[q].wait_ge(T.sem[lab], count[lab])
+            queue[q].wait_ge(sem[lab], count[lab])
             waited[lab] = count[lab]
             for e in members[lab]:
                 know[q] |= ops[e]["know"] | 1 << e
@@ -123,18 +127,21 @@ def _emit(g, T, ops):
             queue[q].wait_ge(T.sem[s], v)
         o["know"] = know[q]
         ins = o["fn"](queue[q])
-        if o["label"] is None:
+        lab = o["label"]
+        if lab is None:
             continue
-        ins.then_inc(T.sem[o["label"]], o["inc"])
-        count[o["label"]] = count.get(o["label"], 0) + o["inc"]
-        members.setdefault(o["label"], []).append(n)
+        if lab not in sem:
+            sem[lab] = T.sem[LOCAL[len(sem)]]
+        ins.then_inc(sem[lab], o["inc"])
+        count[lab] = count.get(lab, 0) + o["inc"]
+        members.setdefault(lab, []).append(n)
         for k in o["r"]:
             readers.setdefault(k, []).append(n)
         for k in o["w"]:
             writer[k], readers[k] = n, []
     for lab in count:
         if waited.get(lab, 0) < count[lab]:
-            g.wait_ge(T.sem[lab], count[lab])
+            g.wait_ge(sem[lab], count[lab])
 
 
 def rank_program(g, core, T, topo):
@@ -202,214 +209,375 @@ def rank_program(g, core, T, topo):
             sent[0] += _write(e, T, topo, core, dst, out, a, sem)
         op("g", None, fn, r)
 
-    def halves(outs, ins, sem, r):
-        def fn(e):
-            xs = []
-            for i, h in enumerate(helpers):
-                rid, pid = topo.addr(h, core)
-                en = topo.engines(core, h)
-                en = en[len(en) // 2 * i:len(en) // 2 * (i + 1)]
-                xs.append(RemoteDMATransfer(dst_ids=[DstId(rid=rid, pnc=pid)], dma_engine_mask=_mask(en), remote_sem=T.sem[sem], src=ins[i], dst=outs))
-                sent[0] += len(en)
-            e.remote_dma_fused(xs, local_sem=T.sem.out)
-        op("g", None, fn, r)
+    def keys(name, a, b):
+        return " ".join("%s%d" % (name, k) for k in range(a, b))
 
     u8 = dt.uint8
 
-    dma("y", "ldx", T.xt[:], T.x[:], w="x0 x1 x2 x3")
-    dma("s", "ldu", T.ut[:], T.u[:], w="ut")
-    iota("gi0", T.uli[:], [[1, 2], [16, 8]], 0, 0, "uli", small=False)
-    iota("gi0", T.pi[:, 0:1], [[1, 1]], 0, 1, "pi0", small=False)
-    iota("gi1", T.tmp[:], [[0, NB], [8, 16]], 4, 0, "tmp")
-    iota("gi2", T.iot[:], [[1, 2 * C]], 0, 0, "iot")
-    iota("gi3", T.tmn[:], [[0, NB], [-8, 16]], 4, 0, "tmn")
-    fill("fill", T.keep[:, 0:SEG], 1.0, "keep")
-    ts("q0", T.pi[:, 1:2], T.pi[:, 0:1], 15, A.bitwise_and, r="pi0", w="pi1")
-    cp("ul", T.ul[:], T.uli[:], "uli", "ul")
-    cp("q1", col(0), T.pi[:, 1:2], "pi1", "c0")
-    fill("q4", T.cap[:], float(CAP), "cap")
-    ts("q2", col(1), col(0), 8.0, A.mult, r="c0", w="c1")
-    ts("q2", col(2), col(0), float(1 - JUNK), A.add, 1.0, A.max, "c0", "c2")
-    ts("q2", col(4), col(0), 15.0, A.is_equal, r="c0", w="c4")
-    ts("keep", T.keepf[:], T.tmp[:, 0:LO], col(1), A.subtract, 4.0, A.not_equal, "tmp c1", "keepf")
-    ts("hot", T.hot[:], T.tmp[:], col(1), A.subtract, 4.0, A.is_equal, "tmp c1", "hot")
-    ts("q3", col(3), col(2), 1.0, A.add, col(2), A.mult, "c2", "c3")
-    ts("q4", col(5), T.pi[:, 0:1], -4.0, A.mult, -2.0, A.add, "pi0", "c5")
-    fill("q4", T.cum[:, 0:1], 0.0, "cum0")
-    fill("q4", T.a16[:, C:C + 1], -TOP, "a16e")
-    fill("q4", T.b16[:, C:C + 1], 0.0, "b16e")
-    ts("q4", T.lists[:, 0:1], col(3), 8.0, A.mult, -1.0, A.add, "c3", "ends")
-    ts("mx", T.mx[:], T.hot[:], -8320.0, A.mult, 128.0, A.add, "hot", "mx")
-    act("kz", T.keep[:, SEG:SEG + HI], T.keepf[:, HI - 1::-1], F.Copy, "keepf", "keepr")
-    for k in range(KV):
-        act("kz", T.keep[:, 8 * k * (k + 1):8 * k * (k + 1) + 16], T.keepf[:, 15::-1], F.Copy, "keepf keep", "keep%d" % k)
-    lin("qs", col(7), col(4), 4.0, -WIPE - 4.0, "c4", "c7")
-    lin("qs", col(8), col(4), -1.0, 1.0, "c4", "c8")
-    lin("qs", col(9), col(0), 1024.0, -15360.0, "c0", "c9")
-    lin("qs", T.ad[:, 0:1], col(4), 0.0, WIPE, "c4", "ad0")
-    lin("qs", T.bd[:, 0:1], col(4), 4.0, -WIPE - 4.0, "c4", "bd0")
-    quant("qu", T.uc[:], T.us[:], T.ut[:], "ut", "uq")
-    cp("pc", T.upc[:].bitcast(dt.uint32), T.uc[:].bitcast(dt.uint32).indirect(T.ul[:]), "uq ul", "upc")
-    act("ps", T.ups[:], T.us[:].indirect(T.ul[:]), F.Copy, "uq ul", "ups")
-    act("ge", T.dist[:], T.iot[:, 0:518], F.Abs, "iot c5", "dist", bias=col(5))
-    ts("cb", T.cb[:], T.tmp[:], col(1), A.subtract, -4.0, A.max, "tmp c1", "cb")
-
-    def send_state(t):
+    def send_state(t, late):
         far = T.cores[rank ^ MASKS[t]]
-        xc, xs, key = T["xc%d" % t], T["xs%d" % t], "xq%d xq%dh" % (t, t)
+        xc, xs, lo, hi = T["xc%d" % t], T["xs%d" % t], "xq%dl" % t, "xq%dh" % t
+        lc, rc = T["lc%d" % t], T["rc%d" % t]
         theirs = [len(topo.engines(h, core)) for h in _helpers(topo, T, rank ^ MASKS[t])]
         if far in topo.cores_of(core):
-            write(helpers[0], T["rs%d" % t][:], xs[:], "hsc%d" % t, key)
-            write(far, T["lc%d" % t][:].bitcast(u8), xc[:].bitcast(u8), "bulk%d" % t, key)
+            if not late:
+                write(helpers[0], T["rs%d" % t][:], xs[:], "hsc%d" % t, lo + " " + hi)
+                write(far, lc[:].bitcast(u8), xc[:].bitcast(u8), "bulk%d" % t, lo + " " + hi)
             return len(topo.engines(far, core)) + theirs[0]
         if not topo.may_write(core, far):
-            write(helpers[0], T["rs%d" % t][:], xs[:], "hsc%d" % t, key)
-            write(helpers[1], T["rc%d" % t][:].bitcast(u8), xc[:].bitcast(u8), "hc%d" % t, key)
-            return sum(theirs)
-        halves(T["rc%d" % t][:, 0:H].bitcast(u8), [xc[:, H * i:H * i + H].bitcast(u8) for i in range(2)], "hc%d" % t, key)
-        halves(T["rs%d" % t][:, 0:H], [xs[:, H * i:H * i + H] for i in range(2)], "hsc%d" % t, key)
-        return 2 * sum(theirs)
+            if not late:
+                write(helpers[1], rc[:, LO:C].bitcast(u8), xc[:, LO:C].bitcast(u8), "hc%d" % t, hi)
+                write(helpers[0], T["rs%d" % t][:], xs[:], "hsc%d" % t, lo + " " + hi)
+                write(helpers[0], rc[:, 0:LO].bitcast(u8), xc[:, 0:LO].bitcast(u8), "hd%d" % t, lo)
+            return 2 * theirs[0] + theirs[1]
+        if not late:
+            write(far, lc[:, LO:C].bitcast(u8), xc[:, LO:C].bitcast(u8), "bulk%d" % t, hi)
+        else:
+            write(far, lc[:, 0:LO].bitcast(u8), xc[:, 0:LO].bitcast(u8), "bulk%d" % t, lo)
+            write(far, T["ls%d" % t][:], xs[:], "bulk%d" % t, lo + " " + hi)
+        return 3 * len(topo.engines(far, core))
 
     def send_table(t):
         far = T.cores[rank ^ MASKS[t]]
-        lm = T["lm%d" % t][:, LM0:LM0 + NB]
+        lm, key = T["lm%d" % t][:, 0:NB], "lm%dl0 lm%dl1 lm%dh0 lm%dh1" % (t, t, t, t)
         if topo.may_write(core, far):
-            write(far, T["tl%d" % t][:], lm, "tab%d" % t, "lma%d lmb%d" % (t, t))
+            write(far, T["tl%d" % t][:], lm, "tab%d" % t, key)
             return len(topo.engines(far, core))
-        write(helpers[0], T.rt[:], lm, "ht%d" % t, "lma%d lmb%d" % (t, t))
+        write(helpers[0], T.rt[:], lm, "ht%d" % t, key)
         return len(topo.engines(_helpers(topo, T, rank ^ MASKS[t])[0], core))
 
-    def own(b):
-        return T.win[:, 2 * C * b:2 * C * b + C]
+    def plane(t, b, a=0, e=2 * C):
+        return T["win%d" % (t % 2)][:, 2 * C * b + a:2 * C * b + e]
+
+    def unit(i):
+        op("g", "gi%d" % i, lambda e: e.affine_select(T.eb[:, 516 * i:516 * i + 516], T.one[:], [[1, 516]], A.is_equal, 0.0, -2 - i, -4), "one", "eb%d" % i)
+
+    def pick(a):
+        o, i = slice(128 * a, 128 * a + 128), T.ul[:, 8 * a:8 * a + 8]
+        cp("pc%d" % a, T.upc[:, o].bitcast(dt.uint32), T.uc[:].bitcast(dt.uint32).indirect(i), "uq ul", "upc%d" % a)
+        act("pz%d" % a, T.ups[:, o], T.us[:].indirect(i), F.Copy, "uq ul", "ups%d" % a)
+
+    def quant_x(t, h):
+        a, e = HALF[h]
+        quant("qx" + h, T["xc%d" % t][:, a:e], T["xs%d" % t][:, a:e], T.xt[:, 4 * a:4 * e], keys("x" + h, 0, 4), "xq%d%s" % (t, h))
+
+    def score(t, label, b, side, a, e):
+        o = slice(128 * side, 128 * side + 128)
+        r = "upc%d ups%d" % (side, side) + (" xq%dl" % t if a < LO else "") + (" xq%dh" % t if e > LO else "")
+        mm(label, b, T.upc[:, o], T.ups[:, o], T["xc%d" % t][:, a:e], T["xs%d" % t][:, a:e], r, n=e - a)
+
+    def mask(h):
+        a, e = HALF[h]
+        b, m = (0, T.hot) if h == "h" else (4, T.hop)
+        tt("sm" + h, T.sm[:, a:e], bank(b, e - a), m[:, 0:e - a], A.mult, "ps%d hot hop" % b, "sm" + h)
+
+    def hold(h):
+        a, e = HALF[h]
+        scan("hs" + h, T.hs[:, a:e], T.keep[:, 0:e - a], T.sm[:, a:e], 0.0, A.mult, A.add, "keep sm" + h, "hs" + h)
+
+    def compare(k, label="cmp"):
+        n, p = 16 * (k + 1), _start(k) + 1
+        if k < KV:
+            ts(label, T.cmp[:, p:p + n], T.ps[:, 2048 + n - 1:2047:-1], T.hs[:, n - 1:n], A.is_lt, -1.0, A.mult, "ps4 hsl", "cmp%d" % k)
+        else:
+            act(label, T.cmp[:, p:p + n], T.ps[:, 512 + n - 1:511:-1], F.Sign, "ps1 hsh", "cmp%d" % k, bias=T.hs[:, n - 1:n])
+
+    def count(h, a, b):
+        k0, n, w, p = PAIRS[h]
+        p, q = p + w * a, p + w * b
+        scan("cs" + h, T.cs[:, p:q], T.cmp[:, p:q], T.dl[:, p:q], 0.0, A.add, A.add,
+             keys("cmp", k0 + a, k0 + b) + " " + keys("cmp", k0 + 2 * n - b, k0 + 2 * n - a) + " cmpx dk", "cs%s%d" % (h, a))
+
+    def table(t, h, q):
+        k0, n, w, p = PAIRS[h]
+        lm, r = T["lm%d" % t], keys("cs" + h, 0, n)
+        for i, (o, a) in enumerate(((lm[:, k0:k0 + n], T.cs[:, p + 16 * k0 + 17:p + w * n:w + 16]),
+                                    (lm[:, k0 + n:k0 + 2 * n], T.cs[:, p + w * n - 1:p:-w]))):
+            if q == "v":
+                ts("lm" + h, o, a, SHIFT, A.add, 0.5, A.mult, r, "lm%d%s%d" % (t, h, i))
+            else:
+                lin("lm" + h, o, a, 0.5, SHIFT / 2, r, "lm%d%s%d" % (t, h, i))
+
+    def addends(h):
+        a, e = HALF[h]
+        i = T.m16[:, a // 16:e // 16]
+        act("a32" + h, T.a32[:, a:e], T.taba[:].indirect(i), F.Copy, "taba m16", "a32" + h)
+        op("g", "a16" + h, lambda g_: g_.affine_select(T.a16[:, a:e], T.a32[:, a:e], [[0, e - a]], A.is_gt, 0.0, 1, 0), "a32" + h, "a16" + h)
+
+    def last(h):
+        a, e = HALF[h]
+        lin("al" + h, T.al[:, a // 16:e // 16], T.a32[:, a + 15:e:16], col(8), 0.0, "c8 a32" + h, "al" + h)
+        lin("al" + h, T.bl[:, a // 16:e // 16], T.a32[:, a + 15:e:16], -1.0, 0.75 * U, "a32" + h, "bl" + h)
+
+    def ad(h):
+        a, e = HALF[h]
+        tt("ad" + h, T.ad[:, a:e], T.taba[:].indirect(T.m16[:, a // 16:e // 16]), T.ca[:, a:e], A.max, "taba m16 ca", "ad" + h)
+
+    def bd(h):
+        a, e = HALF[h]
+        tt("bd" + h, T.bd[:, a:e], T.tabb[:].indirect(T.m16[:, a // 16:e // 16]), T.cb[:, a:e], A.min, "tabb m16 cb", "bd" + h)
+
+    def runs(h):
+        a, e = HALF[h]
+        scan("dout" + h, T.dout[:, a:e - 1], T.ad[:, a:e - 1], T.bd[:, a:e - 1], col(6), A.add, A.add, "c6 ad%s bd%s" % (h, h), "dout" + h)
+
+    def v1(h):
+        a, e = HALF[h]
+        tt("v1" + h, T.v1[:, a // 16:e // 16], T.dout[:, a + 14:e:16], T.al[:, a // 16:e // 16], A.add, "dout%s al%s" % (h, h), "v1" + h)
+
+    def v2(h):
+        a, e = HALF[h]
+        tt("v2" + h, T.v2[:, a // 16:e // 16], T.v1[:, a // 16:e // 16], T.bl[:, a // 16:e // 16], A.add, "v1%s bl%s" % (h, h), "v2" + h)
+
+    def b16(h):
+        a, e = HALF[h]
+        ts("b16" + h, T.b16[:, a:e], T.a16[:, a:e], -1.0, A.mult, 0.75 * U, A.add, "a16" + h, "b16" + h)
+
+    def push(k):
+        a, h = 16 * k + 16, "l" if k < KV else "h"
+        scan("scan" + h, T.o16[:, OW * k + 16 * k:OW * k + OW], T.a16[:, a:C + 1], T.b16[:, a:C + 1], T.v2[:, k:k + 1], A.add, A.add,
+             "a16h b16h a16e v2" + h + (" a16l b16l" if a < LO else ""), "o%d" % k)
+
+    def places(h):
+        a, e = (0, KV) if h == "l" else (KV, NB - 1)
+        if h == "h":
+            ts("plh", T.pl[:, NB - 1:NB], T.v2[:, NB - 1:NB], 0.5 / U, A.mult, C // 2 - TOP * 0.5 / U, A.add, "v2h", "pl7")
+        ts("pl" + h, T.pl[:, a:e], T.o16[:, OW * a + OW - 1:OW * e:OW], 0.5 / U, A.mult, float(C // 2), A.add, keys("o", a, e), "pl" + h)
+
+    def scatter(h):
+        a, e = HALF[h]
+        cp("orow" + h, T.orow[:].indirect(T.pl[:, a // 16:e // 16]), T.name[:, a:e], "pl7 name pl" + h, "orow")
+
+    def oext(h):
+        a, e = HALF[h]
+        scan("oext" + h, T.oext[:, a:e], T.mo[:, a:e], T.orow[:, a:e], 0.0, A.add, A.max, "mo orow", "oext" + h)
+
+    def olist(h):
+        a, e = HALF[h]
+        ts("ol" + h, T.ol[:, a // 16:e // 16], T.oext[:, a + 15:e:16], col(9), A.add, r="c9 oext" + h, w="ol" + h)
+
+    def gather(t, h, b, q):
+        a, e = HALF[h]
+        src, out = plane(t, b).indirect(T.ol[:, a // 16:e // 16]), T.zt[:, 4 * a + b:4 * e:4]
+        r = "own%d%dl own%d%dh far%d ol%s" % (t % 2, b, t % 2, b, b, h)
+        if q == "v":
+            ts("zv" + h, out, src, 0.03125, A.mult, r=r, w="z%s%d" % (h, b))
+        else:
+            act("zs" + h, out, src, F.Copy, r, "z%s%d" % (h, b), scale=0.03125)
+
+    def quant_z(h):
+        a, e = HALF[h]
+        quant("qz" + h, T.zc[:, a:e], T.zs[:, a:e], T.zt[:, 4 * a:4 * e], keys("z" + h, 0, 4), "zq" + h)
+        for b in range(4):
+            mm("r%s%d" % (h, b), b + (4 if h == "l" else 0), T.wq[:, 128 * b:128 * b + 128], T.wp[:, 128 * b:128 * b + 128],
+               T.zc[:, a:e], T.zs[:, a:e], "wq wp zq" + h, n=e - a)
+
+    def z32(h, q):
+        a, e = HALF[h]
+        if q == "v":
+            ts("z3" + h, T.z32[:, 4 * a:4 * e], T.zt[:, 4 * a:4 * e], 32.0, A.mult, r=keys("z" + h, 0, 4), w="y" + h)
+        else:
+            act("z3" + h, T.z32[:, 4 * a:4 * e], T.zt[:, 4 * a:4 * e], F.Copy, keys("z" + h, 0, 4), "y" + h, scale=32.0)
+
+    def add(t, h, b):
+        a, e = HALF[h]
+        k = b + (4 if h == "l" else 0)
+        tt("add%s%d" % (h, b), plane(t + 1, b, a, e), bank(k, e - a), T.z32[:, 4 * a + b:4 * e:4], A.add, "ps%d y%s" % (k, h), "own%d%d%s" % ((t + 1) % 2, b, h))
+
+    def state(t, h, b, q):
+        a, e = HALF[h]
+        r, w = "own%d%d%s" % ((t + 1) % 2, b, h), "x%s%d" % (h, b)
+        if q == "v":
+            ts("xv" + h, T.xt[:, 4 * a + b:4 * e:4], plane(t + 1, b, a, e), 0.03125, A.mult, r=r, w=w)
+        else:
+            act("xs" + h, T.xt[:, 4 * a + b:4 * e:4], plane(t + 1, b, a, e), F.Copy, r, w, scale=0.03125)
+
+    def unpacker(b):
+        a = 516 * (b % 2) + 2 - b // 2 * 2
+        quant("qe", T.ec[:, 128 * b:128 * b + 128], T.es[:, 128 * b:128 * b + 128], T.eb[:, a:a + 512], "eb%d" % (b % 2), "eq%d" % b)
+
+    dma("s", "ldu", T.ut[:], T.u[:], w="ut")
+    dma("y", "ldxh", T.xt[:, 4 * LO:4 * C], T.x[:, 4 * LO:4 * C], w=keys("xh", 0, 4))
+    dma("y", "ldx", T.xt[:, 0:4 * LO], T.x[:, 0:4 * LO], w=keys("xl", 0, 4))
+    iota("gi0", T.pi[:, 0:1], [[1, 1]], 0, 1, "pi0", small=False)
+    iota("gi4", T.uli[:], [[1, 2], [16, 8]], 0, 0, "uli", small=False)
+    iota("gi1", T.tmp[:], [[0, NB], [1, 16]], 0, 0, "tmp")
+    iota("gi2", T.iot[:, 0:C], [[1, C]], 0, 0, "iot")
+    iota("gi3", T.one[:], [[0, 516]], 1, 0, "one")
+    third = TOT // 3
+    fill("fill", T.dl[:, 0:third], 1.5, "dl0")
+    ts("q0", T.pi[:, 1:2], T.pi[:, 0:1], 15, A.bitwise_and, r="pi0", w="pi1")
+    fill("fill", T.dl[:, third:2 * third], 1.5, "dl1")
+    cp("q1", col(0), T.pi[:, 1:2], "pi1", "c0")
+    cp("ul", T.ul[:], T.uli[:], "uli", "ul")
+    fill("fill", T.dl[:, 2 * third:TOT], 1.5, "dl2")
+    fill("pat", T.pat[:, 0:1], -BASE, "pat0")
+    fill("pat", T.pat[:, 1:2], PARK, "pat1")
+    ts("hot", T.hot[:], T.tmp[:], col(0), A.is_equal, -1.0, A.mult, "tmp c0", "hot")
+    lin("qs", col(1), col(0), 1.0, 0.5, "c0", "c1")
+    lin("qs", col(2), col(0), -1.0, 0.5, "c0", "c2")
+    act("qs", col(4), col(0), F.Relu, "c0", "c4", bias=-14.0)
+    lin("mx", T.cap[:], T.tmp[:], 0.0, float(CAP), "tmp", "cap")
+    act("ca", T.ca[:], T.tmp[:], F.Sign, "tmp c1", "ca", scale=-1.0, bias=col(1))
+    act("ca", T.cb[:], T.tmp[:], F.Sign, "tmp c2", "cb", bias=col(2))
+    quant("qu", T.uc[:], T.us[:], T.ut[:], "ut", "uq")
+    ts("pat", T.pat[:, 2:18], T.hot[:, 15::-1], PARK, A.mult, 1.5, A.add, "hot", "pat2")
+    ts("keep", T.keep[:], T.tmp[:, 0:C - LO], col(0), A.not_equal, r="tmp c0", w="keep")
+    pick(0)
+    ts("keep", T.hop[:], T.tmp[:, 0:LO], col(0), A.is_equal, r="tmp c0", w="hop")
+    for k in range(NB):
+        a = 0 if k else 1
+        act("kz", T.dl[:, _start(k) - 1 + a:_start(k) + 17], T.pat[:, a:18], F.Copy, "pat0 pat1 pat2 dl0 dl1 dl2", "dk%d" % k)
+    act("kz", T.dl[:, TOT - 1:TOT], T.pat[:, 0:1], F.Copy, "pat0 dl2", "dk")
+    quant_x(0, "h")
+    for k0, n, w, p in PAIRS.values():
+        for a, step, c in ((0, w, BASE), (16 * k0 + 18, w + 16, BASE), (16 * k0 + 17, w + 16, -SHIFT), (w - 1, w, -SHIFT)):
+            fill("q4", T.cmp[:, p + a:p + w * n:step], c, "cmpx" if k0 and a == w - 1 else "cmpx%d" % (p + a))
+    score(0, "sh", 0, 0, LO, C)
+    quant_x(0, "l")
+    pick(1)
+    mask("h")
 
     for t in range(3):
-        xc, xs, xq = T["xc%d" % t], T["xs%d" % t], "xq%d" % t
-        lmb = T["lm%d" % t]
-        lm, lmk = lmb[:, LM0:LM0 + NB], "lma%d lmb%d" % (t, t)
-        quant("qxh", xc[:, CUT:C], xs[:, CUT:C], T.xt[:, 4 * CUT:4 * C], "x0 x1 x2 x3", xq + "h")
-        quant("qx", xc[:, 0:CUT], xs[:, 0:CUT], T.xt[:, 0:4 * CUT], "x0 x1 x2 x3", xq)
-        mm("sh", 7, T.upc[:, 0:128], T.ups[:, 0:128], xc[:, CUT:C], xs[:, CUT:C], "upc ups %sh" % xq, n=128)
-        xq += " %sh" % xq
-        nbulk = send_state(t)
-        mm("sa", 0, T.upc[:, 0:128], T.ups[:, 0:128], xc[:, 0:LO], xs[:, 0:LO], "upc ups " + xq, n=LO)
-        mm("sb", 1, T.upc[:, 0:128], T.ups[:, 0:128], xc[:], xs[:], "upc ups " + xq)
-        mm("s1", 2, T.upc[:, 128:256], T.ups[:, 128:256], xc[:], xs[:], "upc ups " + xq)
+        lm = T["lm%d" % t]
+        nbulk = send_state(t, False)
         if t == 0:
-            dma("y", "ldw", T.wq[:].bitcast(u8), T.wc[:], "x0", "wq")
-            dma("y", "ldw", T.wp[:], T.ws[:], "", "wp")
-            dma("y", "ldv", T.vt[:], T.v[:], "", "vt")
-        back = T.ps[:, 512 * 7 + 127:512 * 7 + 127 - HI:-1]
-        tt("smh", T.sm[:, LO:C], back, T.hot[:, HI - 1::-1], A.mult, "ps7 hot", "smh")
-        scan("hsh", T.hs[:, LO:C], T.keep[:, SEG:SEG + HI], T.sm[:, LO:C], 0.0, A.mult, A.add, "keepr smh", "hsh")
-        tt("sm", T.sm[:, 0:LO], bank(0, LO), T.hot[:, 0:LO], A.mult, "ps0 hot", "sm")
-        tt("cmp", T.cmp[:, SEG:SEG + HI], back, T.hs[:, LO:C], A.is_ge, "ps7 hsh", "cmpd")
-        scan("hs", T.hs[:, 0:LO], T.keepf[:], T.sm[:, 0:LO], 0.0, A.mult, A.add, "keepf sm", "hs")
+            unit(0)
+        score(t, "sa", 4, 0, 0, LO)
+        score(t, "sb", 1, 0, 0, C)
+        score(t, "s1", 2, 1, 0, C)
+        hold("h")
+        mask("l")
+        for j in range(5):
+            compare(NB - 1 - j, "sg%d" % j)
+            compare(KV + j, "sg%d" % j)
+        if t == 0:
+            fill("q2", T.cum[:, 0:1], 0.0, "cum0")
+            lin("mx", T.mx[:], T.hot[:], 8320.0, 128.0, "hot", "mx")
+        hold("l")
+        ts("wt", T.wt[:], bank(2), 0.0, A.is_gt, r="ps2", w="wt")
         for k in range(KV):
-            n = 16 * (k + 1)
-            ts("cmp", T.cmp[:, 8 * k * (k + 1):8 * k * (k + 1) + n], T.ps[:, n - 1::-1], T.hs[:, n - 1:n], A.is_ge, r="ps0 hs", w="cmp%d" % k)
-        for k in range(KV, NB):
-            n, a, c = 16 * k, C * (k - KV), LO + 16 * (NB - k) - 1
-            act("sg", T.sg[:, a:a + n], bank(1, n), F.Sign, "ps1 hsh", "sg%d" % k, scale=-1.0, bias=T.hs[:, c:c + 1])
-        for k in range(KV, NB):
-            n, a = 16 * k, C * (k - KV)
-            act("acc", T.sr[:, a:a + n], T.sg[:, a:a + n], F.Sign, "sg%d" % k, "acc%d" % k, scale=-1.0, bias=1.0,
-                accum_out=T.acc[:, k - KV:k - KV + 1])
-        scan("cs", T.cs[:], T.keep[:], T.cmp[:], 0.0, A.mult, A.add, "keep keepr cmpd " + " ".join("cmp%d keep%d" % (k, k) for k in range(KV)), "cs")
-        cp("lm", lmb[:, LM0 - JUNK:LM0 + KV], T.cs[:, 0:SEG].indirect(T.lists[:, 0:1]), "cs ends", "lma%d" % t)
-        tt("lm", lmb[:, LM0 + KV:LM0 + NB], T.acc[:], T.cs[:, SEG + HI - 1:SEG:-16], A.add,
-           "cs " + " ".join("acc%d" % k for k in range(KV, NB)), "lmb%d" % t)
+            compare(k)
+        count("h", 0, 2)
+        count("l", 0, 4)
+        for j in range(2, 5):
+            count("h", j, j + 1)
+        table(t, "l", "s")
+        scan("cum", T.cum[:, 1:C + 1], T.wt[:], T.cap[:], 0.0, A.add, A.min, "wt cap", "cum")
+        table(t, "h", "v")
         ntab = send_table(t)
+        send_state(t, True)
         if t == 0:
-            ts("ca", T.ca[:], T.tmn[:], col(1), A.add, 4.0, A.min, "tmn c1", "ca")
-            act("ge2", T.eb[:, 0:516], T.dist[:, 0:516], F.Relu, "dist", "eb", scale=-1.0, bias=1.0)
-            act("ge2", T.eb[:, 517:1032], T.dist[:, 0:515], F.Relu, "dist", "eb2", scale=-1.0, bias=1.0)
-            lin("cs2", T.eb[:, 516:517], col(4), 0.0, 0.0, "c4", "eb3")
-            lin("cs2", T.iod[:], T.iot[:, 0:C:16], 1.0, col(0), "iot c0", "iod")
+            unit(1)
+            lin("qs", col(7), col(4), 1.0, -WIPE - 1.0, "c4", "c7")
+            for a in (0, C):
+                lin("taba", T.taba[:, a:a + C], T.iot[:, 0:C], -2 * U, 289.25 * U, "iot", "taba" if a else "taba0")
+        scan("e1", T.e1[:], T.mx[:], T.cum[:, 1:C + 1], 0.0, A.add, A.max, "mx cum", "e1")
+        scan("e1", T.e2[:], T.mx[:], T.cum[:, 0:C], 0.0, A.add, A.max, "mx cum cum0", "e2")
+        lin("p2", T.p2[:], lm[:, 0:NB], 1.0, float(C), "lm%dl0 lm%dl1 lm%dh0 lm%dh1" % (t, t, t, t), "p2")
+        if t == 0:
+            lin("qs", T.iod[:], T.iot[:, 0:C:16], 1.0, col(0), "iot c0", "iod")
             lin("cs2", T.ca[:, 15:C:16], T.iot[:, 0:NB], 0.0, WIPE, "iot", "ca")
             lin("cs2", T.cb[:, 15:C:16], T.iot[:, 0:NB], 0.0, col(7), "iot c7", "cb")
             for a in (0, C):
-                b = min(a, 1)
-                lin("taba", T.taba[:, a + b:a + C + 1], T.iot[:, b:C + 1], -2 * U, 291.25 * U, "iot", "taba%d" % a)
-                lin("taba", T.tabb[:, a + b:a + C + 1], T.iot[:, b:C + 1], 2 * U, -290.5 * U, "iot", "tabb%d" % a)
-        ts("wt", T.wt[:], bank(2), 0.0, A.is_gt, r="ps2", w="wt")
-        ts("p2", T.p2[:], lm, float(C), A.add, r=lmk, w="p2")
-        scan("cum", T.cum[:, 1:C + 1], T.wt[:], T.cap[:], 0.0, A.add, A.min, "wt cap", "cum")
-        scan("e1", T.e1[:], T.mx[:], T.cum[:, 1:C + 1], 0.0, A.add, A.max, "mx cum", "e1")
-        scan("e2", T.e2[:], T.mx[:], T.cum[:, 0:C], 0.0, A.add, A.max, "mx cum cum0", "e2")
-        tt("take", T.take[:], T.e1[:, 15:C:16], T.e2[:, 15:C:16], A.subtract, "e1 e2", "take")
-        tt("p1", T.p1[:], T.p2[:], T.take[:], A.mult, "take p2", "p1")
-        ts("n1", T.n1[:], T.take[:], float(C), A.mult, r="take", w="n1")
-        tt("p3", T.p3[:], T.p2[:], T.p1[:], A.subtract, "p1 p2", "p3")
-        tt("n2", T.n2[:], T.n1[:], T.iod[:], A.add, "n1 iod", "n2")
-        if t == 0:
-            for b in range(4):
-                a = 516 * (b % 2) + 2 - b // 2 * 2
-                quant("qe", T.ec[:, 128 * b:128 * b + 128], T.es[:, 128 * b:128 * b + 128], T.eb[:, a:a + 512], "eb eb2 eb3", "eq%d" % b)
-        if t == 1:
-            quant("qv", T.vc[:], T.vs[:], T.vt[:], "vt", "vq")
-        cp("n16", T.n16[:], T.n2[:], "n2", "n16")
+                lin("tabb", T.tabb[:, a:a + C], T.iot[:, 0:C], 2 * U, -288.5 * U, "iot", "tabb" if a else "tabb0")
+            lin("qs", col(8), col(4), -1.0, 1.0, "c4", "c8")
+            lin("qs", col(6), col(4), 1.0, TOP - 1.0, "c4", "c6")
+            fill("q2", T.a16[:, C:C + 1], -TOP, "a16e0")
+            fill("q2", T.b16[:, C:C + 1], 0.0, "a16e")
+        tt("own", T.own[:], T.e1[:, 15:C:16], T.e2[:, 15:C:16], A.is_equal, "e1 e2", "own")
+        if t == 2:
+            quant("qu", T.vc[:], T.vs[:], T.vt[:], "vt", "vq")
+        tt("p3", T.p3[:], T.p2[:], T.own[:], A.mult, "own p2", "p3")
+        lin("n1", T.n1[:], T.own[:], -float(C), float(C), "own", "n1")
         tt("mm", T.mm[:], T["tl%d" % t][:], T.p3[:], A.max, "p3", "mm", ext=[("tab%d" % t, ntab)])
-        cp("m16", T.m16[:], T.mm[:], "mm", "m16")
-        act("a32", T.a32[:], T.taba[:].indirect(T.m16[:]), F.Copy, "taba0 taba288 m16", "a32")
-        op("g", "a16", lambda e: e.affine_select(T.a16[:, 0:C], T.a32[:], [[0, C]], A.is_gt, 0.0, 1, 0), "a32", "a16")
-        lin("al", T.al[:], T.a32[:, 15:C:16], col(8), 0.0, "a32 c8", "al")
-        lin("al", T.bl[:], T.a32[:, 15:C:16], -1.0, 0.75 * U, "a32", "bl")
-        act("name", T.name[:], T.iot[:].indirect(T.n16[:]), F.Copy, "iot n16", "name")
         if t == 0:
-            lin("mo", T.mo[:], T.hot[:], -66560.0, 1024.0, "hot", "mo")
+            dma("y", "ldw", T.wq[:].bitcast(u8), T.wc[:], "mm", "wq")
+            dma("y", "ldw", T.wp[:], T.ws[:], "", "wp")
+            unpacker(0)
+        if t == 1:
+            dma("y", "ldu", T.vt[:], T.v[:], "mm", "vt")
+        cp("m16", T.m16[:], T.mm[:], "mm", "m16")
+        tt("n2", T.n2[:], T.n1[:], T.iod[:], A.add, "n1 iod", "n2")
+        addends("h")
+        addends("l")
+        last("h")
+        last("l")
+        ad("h")
+        cp("n16", T.n16[:], T.n2[:], "n2", "n16")
+        if t == 0:
+            lin("taba", T.iot[:, C:2 * C], T.iot[:, 0:C], 1.0, float(C), "iot", "iot2")
+            lin("mx", T.mo[:], T.hot[:], 66560.0, 1024.0, "hot", "mo")
+        act("name", T.name[:], T.iot[:].indirect(T.n16[:]), F.Copy, "iot iot2 n16", "name")
+        if t == 0:
+            lin("mx", col(9), col(0), 1024.0, -15360.0, "c0", "c9")
             for b in range(4):
-                act("w0", own(b), T.xt[:, b:4 * C:4], F.Copy, "x%d" % b, "own%d" % b, scale=32.0)
-        tt("ad", T.ad[:, 1:C + 1], T.taba[:].indirect(T.m16[:]), T.ca[:], A.max, "taba0 taba288 m16 ca", "ad")
-        tt("bd", T.bd[:, 1:C + 1], T.tabb[:].indirect(T.m16[:]), T.cb[:], A.min, "tabb0 tabb288 m16 cb", "bd")
-        scan("dout", T.dout[:], T.ad[:, 0:C], T.bd[:, 0:C], TOP, A.add, A.add, "ad bd ad0 bd0", "dout")
-        tt("v1", T.v1[:], T.dout[:, 15:C:16], T.al[:], A.add, "dout al", "v1")
-        ts("b16", T.b16[:, 0:C], T.a16[:, 0:C], -1.0, A.mult, 0.75 * U, A.add, "a16", "b16")
-        tt("v2", T.v2[:], T.v1[:], T.bl[:], A.add, "v1 bl", "v2")
-        for k in range(NB - 1):
-            a = 16 * k + 16
-            scan("scan", T.o16[:, OW * k + 16 * k:OW * k + OW], T.a16[:, a:C + 1], T.b16[:, a:C + 1], T.v2[:, k:k + 1], A.add, A.add,
-                 "a16 b16 a16e b16e v2", "o%d" % k)
-        ts("pl7", T.pl[:, NB - 1:NB], T.v2[:, NB - 1:NB], 0.5 / U, A.mult, H - TOP * 0.5 / U, A.add, "v2", "pl7")
-        ts("pl", T.pl[:, 0:NB - 1], T.o16[:, OW - 1:OW * (NB - 1):OW], 0.5 / U, A.mult, float(H), A.add, " ".join("o%d" % k for k in range(NB - 1)), "pl")
-        for b in range(4):
-            mm("d%d" % b, 3 + b, T.ec[:, 128 * b:128 * b + 128], T.es[:, 128 * b:128 * b + 128], T["lc%d" % t][:], T["ls%d" % t][:],
+                act("kz", plane(0, b, 0, C), T.xt[:, b:4 * C:4], F.Copy, "xl%d xh%d" % (b, b), "own0%dl own0%dh" % (b, b), scale=32.0)
+        bd("h")
+        ad("l")
+        runs("h")
+        bd("l")
+        v1("h")
+        if t == 0:
+            unpacker(1)
+        runs("l")
+        v2("h")
+        b16("h")
+        v1("l")
+        if t == 0:
+            unpacker(2)
+            unpacker(3)
+        for k in range(NB - 2, KV - 1, -1):
+            push(k)
+            if k == NB - 3:
+                v2("l")
+            if k == NB - 4:
+                b16("l")
+        for k in range(KV - 1, -1, -1):
+            push(k)
+            if k == KV - 3:
+                places("h")
+        for b, k in enumerate((3, 5, 6, 7)):
+            mm("d%d" % b, k, T.ec[:, 128 * b:128 * b + 128], T.es[:, 128 * b:128 * b + 128], T["lc%d" % t][:], T["ls%d" % t][:],
                "eq%d" % b, ext=[("bulk%d" % t, nbulk)] if b == 0 else [])
-        for b in range(4):
-            act("dev", T.win[:, 2 * C * b + C:2 * C * b + 2 * C], bank(3 + b), F.Copy, "ps%d" % (3 + b), "far%d" % b, scale=32.0)
-        cp("orow", T.orow[:].indirect(T.pl[:]), T.name[:], "pl pl7 name", "orow")
-        scan("oext", T.oext[:], T.mo[:], T.orow[:], 0.0, A.add, A.max, "mo orow", "oext")
-        ts("ol", T.ol[:], T.oext[:, 15:C:16], col(9), A.add, r="oext c9", w="ol")
+            act("dev", plane(t, b, C), bank(k), F.Copy, "ps%d" % k, "far%d" % b, scale=32.0)
+        scatter("h")
+        places("l")
+        scatter("l")
+        oext("h")
+        oext("l")
+        olist("h")
+        olist("l")
         if t == 2:
             dma("y", "sto", T.od[:], T.orow[0:128:16, :], "orow")
-        for b in range(4):
-            src, key = T.win[:, 2 * C * b:2 * C * b + 2 * C].indirect(T.ol[:]), "own%d far%d ol" % (b, b)
-            if b < 2:
-                ts("zv", T.zt[:, b:4 * C:4], src, 0.03125, A.mult, r=key, w="z%d" % b)
+        for w in LAYER:
+            step, h = w[0], w[1]
+            if step == "g":
+                gather(t, h, int(w[2]), w[3])
+            elif step == "q":
+                quant_z(h)
+            elif step == "z":
+                z32(h, w[2])
+            elif step == "a":
+                add(t, h, int(w[2]))
+            elif step == "x":
+                state(t, h, int(w[2]), w[3])
+            elif step == "Q":
+                quant_x(t + 1, h)
+                if h == "h" and t < 2:
+                    score(t + 1, "sh", 0, 0, LO, C)
+                elif h == "h":
+                    mm("sh", 0, T.vc[:], T.vs[:], T.xc3[:, LO:C], T.xs3[:, LO:C], "vq xq3h", n=C - LO)
+            elif t < 2:
+                mask(h)
             else:
-                act("zs", T.zt[:, b:4 * C:4], src, F.Copy, key, "z%d" % b, scale=0.03125)
-        quant("qz", T.zc[:], T.zs[:], T.zt[:], "z0 z1 z2 z3", "zq")
-        for b in range(4):
-            if b < 2:
-                ts("z3v", T.z32[:, C * b:C * b + C], T.zt[:, b:4 * C:4], 32.0, A.mult, r="z%d" % b, w="y%d" % b)
-            else:
-                act("z3s", T.z32[:, C * b:C * b + C], T.zt[:, b:4 * C:4], F.Copy, "z%d" % b, "y%d" % b, scale=32.0)
-        for b in range(4):
-            mm("r%d" % b, 3 + b, T.wq[:, 128 * b:128 * b + 128], T.wp[:, 128 * b:128 * b + 128], T.zc[:], T.zs[:], "wq wp zq")
-        for b in range(4):
-            tt("add%d" % b, own(b), bank(3 + b), T.z32[:, C * b:C * b + C], A.add, "ps%d y%d" % (3 + b, b), "own%d" % b)
-        for b in range(3):
-            act("xs", T.xt[:, b:4 * C:4], own(b), F.Copy, "own%d" % b, "x%d" % b, scale=0.03125)
-        ts("xv", T.xt[:, 3:4 * C:4], own(3), 0.03125, A.mult, r="own3", w="x3")
+                act("xsh", T.ysb[:, LO:C], bank(0, C - LO), F.Copy, "ps0", "ysbh")
 
-    quant("qxh", T.xc3[:, 0:H], T.xs3[:, 0:H], T.xt[:, 0:4 * H], "x0 x1 x2 x3", "xq3h")
-    quant("qx", T.xc3[:, H:C], T.xs3[:, H:C], T.xt[:, 4 * H:4 * C], "x0 x1 x2 x3", "xq3")
-    mm("ym", 0, T.vc[:], T.vs[:], T.xc3[:, 0:H], T.xs3[:, 0:H], "vq xq3h", n=H)
-    mm("ym1", 1, T.vc[:], T.vs[:], T.xc3[:, H:C], T.xs3[:, H:C], "vq xq3", n=H)
-    cp("yc", T.ysb[:, 0:H], bank(0, H), "ps0", "ysb")
-    act("yc1", T.ysb[:, H:C], bank(1, H), F.Copy, "ps1", "ysb1")
-    dma("y", "sto", T.oc[:], T.xc3[:].bitcast(u8), "xq3 xq3h")
-    dma("y", "sto", T.y[:], T.ysb[:], "ysb ysb1")
+    mm("sa", 4, T.vc[:], T.vs[:], T.xc3[:, 0:LO], T.xs3[:, 0:LO], "vq xq3l", n=LO)
+    dma("y", "sto", T.oc[:], T.xc3[:].bitcast(u8), "xq3l xq3h")
+    cp("sml", T.ysb[:, 0:LO], bank(4, LO), "ps4", "ysbl")
+    dma("y", "sto", T.y[:], T.ysb[:], "ysbl ysbh")
     for k in range(4):
-        dma("s", "sts", T.osc[4 * k:4 * k + 4, :], T.xs3[32 * k:32 * k + 4, :], "xq3 xq3h")
+        dma("s", "sts", T.osc[4 * k:4 * k + 4, :], T.xs3[32 * k:32 * k + 4, :], "xq3l xq3h")
     _emit(g, T, ops)
     g.wait_ge(T.sem.out, sent[0])

@@ -5,9 +5,15 @@ MASKS = [1, 2, 4]
 KV = 8
 LO = 16 * KV
 HALF = {"h": (LO, C), "l": (0, LO)}
+MINE = {"h": 3, "l": 2}
 PAIRS = {"l": (0, KV // 2, 16 * (KV + 1) + 4, 0), "h": (KV, (NB - KV) // 2, 16 * (NB + KV + 1) + 4, (16 * (KV + 1) + 4) * KV // 2)}
 TOT = PAIRS["h"][3] + PAIRS["h"][1] * PAIRS["h"][2]
-LAYER = ("gh0v gh2s gh1v gh3s gl0v gl2s gl3s gl1s qh zhv ql zls ah0 xh0s ah1 xh1s ah2 xh2s ah3 xh3s "
+ORDER = """hold.h compare.17.16 mask.l compare.8.9.10 compare.15 compare.14.11 wanted hold.l count.h.0.2 count.h.2.3 sums compare.13.12
+count.h.3.4 count.h.4.5 compare.7.6.5.4.3.2 compare.0.1 once.0 unpacker.0 table.h.v send.h once.1 shifted.h count.l.0.4 counted
+table.l.s send.l once.2 unpacker.2 vtile owned kept.h mix.h shifted.l m16.h n1 once.3 kept.l ad.h n2 addends.h mix.l runs.h m16.l
+unpacker.1 last.h v1.h ad.l addends.l v2.h last.l a16.h n16 once.4 runs.l name push.14.17 loads once.5 v1.l unpacker.3 push.8.11
+v2.l a16.l unpack push.11.14 push.5.8 places.8.18 push.0.5 scatter.8.18 places.0.8 scatter.0.8 oext.h oext.l olist.h olist.l""".split()
+LAYER = ("gh0v gh2s gh1v gh3s gl0v gl2s gl3s qh gl1v zh0v zh1v zh2s zh3s ql zl4s ah0 xh0s ah1 xh1s ah2 xh2s ah3 xh3s "
          "al0 al1 al2 al3 xl0s xl1s xl2s Qh xl3v Ql mh").split()
 U = 2.0 ** -10
 TOP = 2.0 ** 14
@@ -24,6 +30,10 @@ def _start(k):
     return p + (w * j if j < n else (w + 16) * (2 * n - 1 - j) + 16 * k0 + 18)
 
 
+def _lst(h):
+    return slice(HALF[h][0] // 16, HALF[h][1] // 16)
+
+
 F32, BF, F16, U16, I32, Q4, U8 = "float32", "bfloat16", "float16", "uint16", "int32", "float8_e4m3fn_x4", "uint8"
 
 
@@ -38,18 +48,18 @@ SCRATCH = {
     "uc": _sb(128, Q4), "us": _sb(128, U8), "upc": _sb(256, Q4), "ups": _sb(256, U8),
     "vc": _sb(128, Q4), "vs": _sb(128, U8), "ec": _sb(512, Q4), "es": _sb(512, U8),
     "wq": _sb(512, Q4), "wp": _sb(512, U8), "zc": _sb(C, Q4), "zs": _sb(C, U8),
-    "one": _sb(516, BF), "eb": _sb(1032, BF),
+    "eb": _sb(1032, BF),
     "uli": _sb(16, I32), "ul": _sb(16, U16), "pi": _sb(2, I32), "cc": _sb(16, F32),
-    "iot": _sb(2 * C, F32), "tmp": _sb(C, BF), "hot": _sb(C, BF), "hop": _sb(LO, BF), "keep": _sb(C - LO, BF),
-    "mx": _sb(C, BF), "mo": _sb(C, F32), "cap": _sb(C, BF), "iod": _sb(NB, F32),
-    "taba": _sb(2 * C, F32), "tabb": _sb(2 * C, F32), "ca": _sb(C, BF), "cb": _sb(C, F32),
+    "iot": _sb(2 * C, F32), "tmp": _sb(C, BF), "hot": _sb(C, BF), "hop": _sb(C, BF), "keep": _sb(C - LO, BF),
+    "mx": _sb(C, BF), "mo": _sb(C, F32), "one": _sb(516, BF), "iod": _sb(NB, F32),
+    "taba": _sb(2 * C, F32), "tabb": _sb(2 * C, F32), "ca": _sb(C, BF),
     "sm": _sb(C, F32), "hs": _sb(C, F32), "cmp": _sb(TOT, BF), "cs": _sb(TOT, BF), "dl": _sb(TOT, BF), "pat": _sb(18, BF),
     "wt": _sb(C, F16), "cum": _sb(C + 2, F16), "e1": _sb(C, F16), "e2": _sb(C, F16),
     "own": _sb(NB, F32), "n1": _sb(NB, F32), "n2": _sb(NB, F32), "n16": _sb(NB, U16), "name": _sb(C, F32),
     "p2": _sb(NB, F32), "p3": _sb(NB, F32),
     "mm": _sb(NB, F32), "m16": _sb(NB, U16),
-    "a32": _sb(C, F32), "ad": _sb(C, F32), "bd": _sb(C, F32), "dout": _sb(C, F32),
-    "al": _sb(NB, F32), "bl": _sb(NB, F32), "v1": _sb(NB, F32), "v2": _sb(NB, F32),
+    "b32": _sb(C, F32), "ad": _sb(C, F32), "dout": _sb(C, F32),
+    "al": _sb(NB, F32), "v1": _sb(NB, F32), "v2": _sb(NB, F32),
     "a16": _sb(C + 2, F16), "b16": _sb(C + 2, F16), "o16": _sb((NB - 1) * OW, F16), "pl": _sb(NB, U16),
     "orow": _sb(C, F32), "oext": _sb(C, F32), "ol": _sb(NB, U16), "ysb": _sb(C, F32),
     "rt": _sb(NB, F32),
@@ -65,8 +75,8 @@ for _t in range(3):
     SCRATCH["lm%d" % _t] = _sb(NB + 2, F32)
     SCRATCH["tl%d" % _t] = _sb(NB, F32)
 
-LOCAL = ["s%d" % _t for _t in range(130)]
-SEMAPHORES = LOCAL + ["out"] + ["%s%d" % (n, t) for n in ("bulk", "tab", "hc", "hd", "hsc", "ht") for t in range(3)]
+LOCAL = ["s%d" % _t for _t in range(133)]
+SEMAPHORES = LOCAL + ["out", "hc", "hd", "hth", "htl"] + ["%s%d" % (n, t) for n in ("bulk", "tabh", "tabl", "hsc") for t in range(3)]
 
 
 def _helpers(topo, T, r):
@@ -93,12 +103,13 @@ def _helper_program(g, core, T, topo, r, i):
             g.wait_ge(T.sem["hsc%d" % t], n)
             sent += _write(g, T, topo, core, far, T["ls%d" % t][:], T["rs%d" % t][:], "bulk%d" % t)
         if i == 0 and hop:
-            g.wait_ge(T.sem["ht%d" % t], n)
-            sent += _write(g, T, topo, core, far, T["tl%d" % t][:], T.rt[:], "tab%d" % t)
-            g.wait_ge(T.sem["hd%d" % t], n)
+            for h in "hl":
+                g.wait_ge(T.sem["ht" + h], n)
+                sent += _write(g, T, topo, core, far, T["tl%d" % t][:, _lst(h)], T.rt[:, _lst(h)], "tab%s%d" % (h, t))
+            g.wait_ge(T.sem.hd, n)
             sent += _write(g, T, topo, core, far, lc[:, 0:LO].bitcast(u8), rc[:, 0:LO].bitcast(u8), "bulk%d" % t)
         if i == 1 and hop:
-            g.wait_ge(T.sem["hc%d" % t], n)
+            g.wait_ge(T.sem.hc, n)
             sent += _write(g, T, topo, core, far, lc[:, LO:C].bitcast(u8), rc[:, LO:C].bitcast(u8), "bulk%d" % t)
     g.wait_ge(T.sem.out, sent)
 
@@ -226,9 +237,9 @@ def rank_program(g, core, T, topo):
             return len(topo.engines(far, core)) + theirs[0]
         if not topo.may_write(core, far):
             if not late:
-                write(helpers[1], rc[:, LO:C].bitcast(u8), xc[:, LO:C].bitcast(u8), "hc%d" % t, hi)
+                write(helpers[1], rc[:, LO:C].bitcast(u8), xc[:, LO:C].bitcast(u8), "hc", hi)
                 write(helpers[0], T["rs%d" % t][:], xs[:], "hsc%d" % t, lo + " " + hi)
-                write(helpers[0], rc[:, 0:LO].bitcast(u8), xc[:, 0:LO].bitcast(u8), "hd%d" % t, lo)
+                write(helpers[0], rc[:, 0:LO].bitcast(u8), xc[:, 0:LO].bitcast(u8), "hd", lo)
             return 2 * theirs[0] + theirs[1]
         if not late:
             write(far, lc[:, LO:C].bitcast(u8), xc[:, LO:C].bitcast(u8), "bulk%d" % t, hi)
@@ -237,25 +248,63 @@ def rank_program(g, core, T, topo):
             write(far, T["ls%d" % t][:], xs[:], "bulk%d" % t, lo + " " + hi)
         return 3 * len(topo.engines(far, core))
 
-    def send_table(t):
-        far = T.cores[rank ^ MASKS[t]]
-        lm, key = T["lm%d" % t][:, 0:NB], "lm%dl0 lm%dl1 lm%dh0 lm%dh1" % (t, t, t, t)
+    def send(t, h):
+        far, lm, key = T.cores[rank ^ MASKS[t]], T["lm%d" % t][:, _lst(h)], keys("lm%d%s" % (t, h), 0, 2)
         if topo.may_write(core, far):
-            write(far, T["tl%d" % t][:], lm, "tab%d" % t, key)
-            return len(topo.engines(far, core))
-        write(helpers[0], T.rt[:], lm, "ht%d" % t, key)
-        return len(topo.engines(_helpers(topo, T, rank ^ MASKS[t])[0], core))
+            write(far, T["tl%d" % t][:, _lst(h)], lm, "tab%s%d" % (h, t), key)
+        else:
+            write(helpers[0], T.rt[:, _lst(h)], lm, "ht" + h, key)
+        if h == "l":
+            send_state(t, True)
+            if t == 0:
+                unit(1)
 
-    def plane(t, b, a=0, e=2 * C):
-        return T["win%d" % (t % 2)][:, 2 * C * b + a:2 * C * b + e]
+    def loads(t):
+        if t == 0:
+            dma("y", "ldw", T.wq[:].bitcast(u8), T.wc[:], "mml", "wq")
+            dma("y", "ldw", T.wp[:], T.ws[:], "", "wp")
+        if t == 1:
+            dma("y", "ldu", T.vt[:], T.v[:], "mml", "vt")
 
     def unit(i):
         op("g", "gi%d" % i, lambda e: e.affine_select(T.eb[:, 516 * i:516 * i + 516], T.one[:], [[1, 516]], A.is_equal, 0.0, -2 - i, -4), "one", "eb%d" % i)
+
+    def unpacker(b):
+        a = 516 * (b % 2) + 2 - b // 2 * 2
+        quant("qe", T.ec[:, 128 * b:128 * b + 128], T.es[:, 128 * b:128 * b + 128], T.eb[:, a:a + 512], "eb%d" % (b % 2), "eq%d" % b)
 
     def pick(a):
         o, i = slice(128 * a, 128 * a + 128), T.ul[:, 8 * a:8 * a + 8]
         cp("pc%d" % a, T.upc[:, o].bitcast(dt.uint32), T.uc[:].bitcast(dt.uint32).indirect(i), "uq ul", "upc%d" % a)
         act("pz%d" % a, T.ups[:, o], T.us[:].indirect(i), F.Copy, "uq ul", "ups%d" % a)
+
+    def signed(h):
+        a, e = HALF[h]
+        c = a + 16 * MINE[h]
+        ts("hop", T.hop[:, a:c], T.tmp[:, a:c], col(0), A.is_equal, r="tmp c0", w="hop" + h)
+        ts("hop", T.hop[:, c:e], T.tmp[:, c:e], col(0), A.is_equal, -1.0, A.mult, "tmp c0", "hoq" + h)
+
+    def once(i):
+        if i == 0:
+            lin("mx", T.mx[:], T.hot[:], 65.0, 1.0, "hot", "mx")
+        if i == 1:
+            for a in (0, C):
+                lin("taba", T.taba[:, a:a + C], T.iot[:, 0:C], -2 * U, 289.25 * U, "iot", "taba" if a else "taba0")
+            lin("ca", T.ca[:], T.hot[:], WIPE, 0.0, "hot", "ca")
+        if i == 2:
+            lin("ca", T.ca[:, 15:C:16], T.hot[:, 15:C:16], WIPE, WIPE, "hot", "ca")
+            for a in (0, C):
+                lin("tabb", T.tabb[:, a:a + C], T.iot[:, 0:C], 2 * U, -288.5 * U, "iot", "tabb" if a else "tabb0")
+            lin("qs", T.iod[:], T.iot[:, 0:C:16], 1.0, col(0), "iot c0", "iod")
+        if i == 3:
+            fill("q1", T.a16[:, C:C + 1], -TOP, "a16e0")
+            fill("q1", T.b16[:, C:C + 1], 0.0, "a16e")
+        if i == 4:
+            lin("taba", T.iot[:, C:2 * C], T.iot[:, 0:C], 1.0, float(C), "iot", "iot2")
+            lin("mx", T.mo[:], T.hot[:], 66560.0, 1024.0, "hot", "mo")
+        if i == 5:
+            for b in range(4):
+                act("kz", plane(0, b, 0, C), T.xt[:, b:4 * C:4], F.Copy, "xl%d xh%d" % (b, b), "own0%dl own0%dh" % (b, b), scale=32.0)
 
     def quant_x(t, h):
         a, e = HALF[h]
@@ -268,25 +317,26 @@ def rank_program(g, core, T, topo):
 
     def mask(h):
         a, e = HALF[h]
-        b, m = (0, T.hot) if h == "h" else (4, T.hop)
-        tt("sm" + h, T.sm[:, a:e], bank(b, e - a), m[:, 0:e - a], A.mult, "ps%d hot hop" % b, "sm" + h)
+        b = 0 if h == "h" else 4
+        tt("sm" + h, T.sm[:, a:e], bank(b, e - a), T.hop[:, a:e], A.mult, "ps%d hop%s hoq%s" % (b, h, h), "sm" + h)
 
     def hold(h):
         a, e = HALF[h]
         scan("hs" + h, T.hs[:, a:e], T.keep[:, 0:e - a], T.sm[:, a:e], 0.0, A.mult, A.add, "keep sm" + h, "hs" + h)
 
-    def compare(k, label="cmp"):
-        n, p = 16 * (k + 1), _start(k) + 1
-        if k < KV:
-            ts(label, T.cmp[:, p:p + n], T.ps[:, 2048 + n - 1:2047:-1], T.hs[:, n - 1:n], A.is_lt, -1.0, A.mult, "ps4 hsl", "cmp%d" % k)
-        else:
-            act(label, T.cmp[:, p:p + n], T.ps[:, 512 + n - 1:511:-1], F.Sign, "ps1 hsh", "cmp%d" % k, bias=T.hs[:, n - 1:n])
+    def compare(*ks):
+        for k in ks:
+            n, p, h = 16 * (k + 1), _start(k) + 1, "l" if k < KV else "h"
+            if k - PAIRS[h][0] < MINE[h]:
+                ts("cmp%d" % ks[0], T.cmp[:, p:p + n], T.ps[:, 2048 + n - 1:2047:-1], T.hs[:, n - 1:n], A.is_lt, -1.0, A.mult, "ps4 hs" + h, "cmp%d" % k)
+            else:
+                act("cmp%d" % ks[0], T.cmp[:, p:p + n], T.ps[:, 512 + n - 1:511:-1], F.Sign, "ps1 hs" + h, "cmp%d" % k, bias=T.hs[:, n - 1:n])
 
     def count(h, a, b):
         k0, n, w, p = PAIRS[h]
         p, q = p + w * a, p + w * b
         scan("cs" + h, T.cs[:, p:q], T.cmp[:, p:q], T.dl[:, p:q], 0.0, A.add, A.add,
-             keys("cmp", k0 + a, k0 + b) + " " + keys("cmp", k0 + 2 * n - b, k0 + 2 * n - a) + " cmpx dk", "cs%s%d" % (h, a))
+             keys("cmp", k0 + a, k0 + b) + " " + keys("cmp", k0 + 2 * n - b, k0 + 2 * n - a) + " dk cmpx", "cs%s%d" % (h, a))
 
     def table(t, h, q):
         k0, n, w, p = PAIRS[h]
@@ -298,55 +348,88 @@ def rank_program(g, core, T, topo):
             else:
                 lin("lm" + h, o, a, 0.5, SHIFT / 2, r, "lm%d%s%d" % (t, h, i))
 
+    def wanted():
+        ts("wt", T.wt[:], bank(2), 0.0, A.is_gt, 1.0 / CAP, A.mult, "ps2", "wt")
+
+    def sums():
+        scan("cum", T.cum[:, 1:C + 1], T.wt[:], T.one[:, 0:C], 0.0, A.add, A.min, "wt one", "cum")
+
+    def counted():
+        scan("e1", T.e1[:], T.mx[:], T.cum[:, 1:C + 1], 0.0, A.add, A.max, "mx cum", "e1")
+        scan("e1", T.e2[:], T.mx[:], T.cum[:, 0:C], 0.0, A.add, A.max, "mx cum cum0", "e2")
+
+    def owned():
+        tt("own", T.own[:], T.e1[:, 15:C:16], T.e2[:, 15:C:16], A.is_equal, "e1 e2", "own")
+
+    def shifted(t, h):
+        lin("p2" + h, T.p2[:, _lst(h)], T["lm%d" % t][:, _lst(h)], 1.0, float(C), keys("lm%d%s" % (t, h), 0, 2), "p2" + h)
+
+    def kept(h):
+        tt("p3" + h, T.p3[:, _lst(h)], T.p2[:, _lst(h)], T.own[:, _lst(h)], A.mult, "own p2" + h, "p3" + h)
+
+    def n1():
+        lin("n1", T.n1[:], T.own[:], -float(C), float(C), "own", "n1")
+
+    def n2():
+        tt("n2", T.n2[:], T.n1[:], T.iod[:], A.add, "n1 iod", "n2")
+
+    def n16():
+        cp("n16", T.n16[:], T.n2[:], "n2", "n16")
+
+    def name():
+        act("name", T.name[:], T.iot[:].indirect(T.n16[:]), F.Copy, "iot iot2 n16", "name")
+
+    def mix(t, h):
+        far = T.cores[rank ^ MASKS[t]]
+        n = len(topo.engines(far if topo.may_write(far, core) else _helpers(topo, T, rank ^ MASKS[t])[0], core))
+        tt("mm" + h, T.mm[:, _lst(h)], T["tl%d" % t][:, _lst(h)], T.p3[:, _lst(h)], A.max, "p3" + h, "mm" + h, ext=[("tab%s%d" % (h, t), n)])
+
+    def m16(h):
+        cp("m16" + h, T.m16[:, _lst(h)], T.mm[:, _lst(h)], "mm" + h, "m16" + h)
+
     def addends(h):
         a, e = HALF[h]
-        i = T.m16[:, a // 16:e // 16]
-        act("a32" + h, T.a32[:, a:e], T.taba[:].indirect(i), F.Copy, "taba m16", "a32" + h)
-        op("g", "a16" + h, lambda g_: g_.affine_select(T.a16[:, a:e], T.a32[:, a:e], [[0, e - a]], A.is_gt, 0.0, 1, 0), "a32" + h, "a16" + h)
+        act("b32" + h, T.b32[:, a:e], T.tabb[:].indirect(T.m16[:, _lst(h)]), F.Copy, "tabb m16" + h, "b32" + h)
+        op("g", "b16" + h, lambda g_: g_.affine_select(T.b16[:, a:e], T.b32[:, a:e], [[0, e - a]], A.is_gt, 0.0, 1, 0), "b32" + h, "b16" + h)
 
     def last(h):
         a, e = HALF[h]
-        lin("al" + h, T.al[:, a // 16:e // 16], T.a32[:, a + 15:e:16], col(8), 0.0, "c8 a32" + h, "al" + h)
-        lin("al" + h, T.bl[:, a // 16:e // 16], T.a32[:, a + 15:e:16], -1.0, 0.75 * U, "a32" + h, "bl" + h)
+        lin("al" + h, T.al[:, _lst(h)], T.b32[:, a + 15:e:16], col(8), col(6), "c6 c8 b32" + h, "al" + h)
 
     def ad(h):
         a, e = HALF[h]
-        tt("ad" + h, T.ad[:, a:e], T.taba[:].indirect(T.m16[:, a // 16:e // 16]), T.ca[:, a:e], A.max, "taba m16 ca", "ad" + h)
-
-    def bd(h):
-        a, e = HALF[h]
-        tt("bd" + h, T.bd[:, a:e], T.tabb[:].indirect(T.m16[:, a // 16:e // 16]), T.cb[:, a:e], A.min, "tabb m16 cb", "bd" + h)
+        tt("ad" + h, T.ad[:, a:e], T.taba[:].indirect(T.m16[:, _lst(h)]), T.ca[:, a:e], A.add, "taba ca m16" + h, "ad" + h)
 
     def runs(h):
         a, e = HALF[h]
-        scan("dout" + h, T.dout[:, a:e - 1], T.ad[:, a:e - 1], T.bd[:, a:e - 1], col(6), A.add, A.add, "c6 ad%s bd%s" % (h, h), "dout" + h)
+        scan("dout" + h, T.dout[:, a:e - 1], T.ad[:, a:e - 1], T.b32[:, a:e - 1], TOP + WIPE, A.add, A.add, "ad%s b32%s" % (h, h), "dout" + h)
 
     def v1(h):
         a, e = HALF[h]
-        tt("v1" + h, T.v1[:, a // 16:e // 16], T.dout[:, a + 14:e:16], T.al[:, a // 16:e // 16], A.add, "dout%s al%s" % (h, h), "v1" + h)
+        tt("v1" + h, T.v1[:, _lst(h)], T.dout[:, a + 14:e:16], T.al[:, _lst(h)], A.add, "dout%s al%s" % (h, h), "v1" + h)
 
     def v2(h):
         a, e = HALF[h]
-        tt("v2" + h, T.v2[:, a // 16:e // 16], T.v1[:, a // 16:e // 16], T.bl[:, a // 16:e // 16], A.add, "v1%s bl%s" % (h, h), "v2" + h)
+        tt("v2" + h, T.v2[:, _lst(h)], T.v1[:, _lst(h)], T.b32[:, a + 15:e:16], A.add, "v1%s b32%s" % (h, h), "v2" + h)
 
-    def b16(h):
+    def a16(h):
         a, e = HALF[h]
-        ts("b16" + h, T.b16[:, a:e], T.a16[:, a:e], -1.0, A.mult, 0.75 * U, A.add, "a16" + h, "b16" + h)
+        ts("a16" + h, T.a16[:, a:e], T.b16[:, a:e], -1.0, A.mult, 0.75 * U, A.add, "b16" + h, "a16" + h)
 
-    def push(k):
-        a, h = 16 * k + 16, "l" if k < KV else "h"
-        scan("scan" + h, T.o16[:, OW * k + 16 * k:OW * k + OW], T.a16[:, a:C + 1], T.b16[:, a:C + 1], T.v2[:, k:k + 1], A.add, A.add,
-             "a16h b16h a16e v2" + h + (" a16l b16l" if a < LO else ""), "o%d" % k)
+    def push(k0, k1):
+        for k in range(k1 - 1, k0 - 1, -1):
+            a = 16 * k + 16
+            scan("scanl" if k < KV else "scanh", T.o16[:, OW * k + 16 * k:OW * k + OW], T.a16[:, a:C + 1], T.b16[:, a:C + 1], T.v2[:, k:k + 1],
+                 A.add, A.add, "a16h b16h a16e v2" + ("l" if k < KV else "h") + (" a16l b16l" if a < LO else ""), "o%d" % k)
 
-    def places(h):
-        a, e = (0, KV) if h == "l" else (KV, NB - 1)
-        if h == "h":
-            ts("plh", T.pl[:, NB - 1:NB], T.v2[:, NB - 1:NB], 0.5 / U, A.mult, C // 2 - TOP * 0.5 / U, A.add, "v2h", "pl7")
-        ts("pl" + h, T.pl[:, a:e], T.o16[:, OW * a + OW - 1:OW * e:OW], 0.5 / U, A.mult, float(C // 2), A.add, keys("o", a, e), "pl" + h)
+    def places(a, e):
+        if e == NB:
+            e -= 1
+            ts("pl%d" % a, T.pl[:, e:NB], T.v2[:, e:NB], 0.5 / U, A.mult, C // 2 - TOP * 0.5 / U, A.add, "v2h", "pl%d" % e)
+        ts("pl%d" % a, T.pl[:, a:e], T.o16[:, OW * a + OW - 1:OW * e:OW], 0.5 / U, A.mult, float(C // 2), A.add, keys("o", a, e), keys("pl", a, e))
 
-    def scatter(h):
-        a, e = HALF[h]
-        cp("orow" + h, T.orow[:].indirect(T.pl[:, a // 16:e // 16]), T.name[:, a:e], "pl7 name pl" + h, "orow")
+    def scatter(a, e):
+        cp("orow", T.orow[:].indirect(T.pl[:, a:e]), T.name[:, 16 * a:16 * e], "name " + keys("pl", a, e), "orow")
 
     def oext(h):
         a, e = HALF[h]
@@ -354,11 +437,20 @@ def rank_program(g, core, T, topo):
 
     def olist(h):
         a, e = HALF[h]
-        ts("ol" + h, T.ol[:, a // 16:e // 16], T.oext[:, a + 15:e:16], col(9), A.add, r="c9 oext" + h, w="ol" + h)
+        ts("ol" + h, T.ol[:, _lst(h)], T.oext[:, a + 15:e:16], col(9), A.add, r="c9 oext" + h, w="ol" + h)
+
+    def plane(t, b, a=0, e=2 * C):
+        return T["win%d" % (t % 2)][:, 2 * C * b + a:2 * C * b + e]
+
+    def unpack(t, n):
+        for b, k in enumerate((3, 5, 6, 7)):
+            mm("d%d" % b, k, T.ec[:, 128 * b:128 * b + 128], T.es[:, 128 * b:128 * b + 128], T["lc%d" % t][:], T["ls%d" % t][:],
+               "eq%d" % b, ext=[("bulk%d" % t, n)] if b == 0 else [])
+            act("dev", plane(t, b, C), bank(k), F.Copy, "ps%d" % k, "far%d" % b, scale=32.0)
 
     def gather(t, h, b, q):
         a, e = HALF[h]
-        src, out = plane(t, b).indirect(T.ol[:, a // 16:e // 16]), T.zt[:, 4 * a + b:4 * e:4]
+        src, out = plane(t, b).indirect(T.ol[:, _lst(h)]), T.zt[:, 4 * a + b:4 * e:4]
         r = "own%d%dl own%d%dh far%d ol%s" % (t % 2, b, t % 2, b, b, h)
         if q == "v":
             ts("zv" + h, out, src, 0.03125, A.mult, r=r, w="z%s%d" % (h, b))
@@ -372,17 +464,19 @@ def rank_program(g, core, T, topo):
             mm("r%s%d" % (h, b), b + (4 if h == "l" else 0), T.wq[:, 128 * b:128 * b + 128], T.wp[:, 128 * b:128 * b + 128],
                T.zc[:, a:e], T.zs[:, a:e], "wq wp zq" + h, n=e - a)
 
-    def z32(h, q):
+    def z32(h, b, q):
         a, e = HALF[h]
+        o, p = (slice(4 * a + b, 4 * e, 4), (b, b + 1)) if b < 4 else (slice(4 * a, 4 * e), (0, 4))
         if q == "v":
-            ts("z3" + h, T.z32[:, 4 * a:4 * e], T.zt[:, 4 * a:4 * e], 32.0, A.mult, r=keys("z" + h, 0, 4), w="y" + h)
+            ts("z3%s%d" % (h, b), T.z32[:, o], T.zt[:, o], 32.0, A.mult, r=keys("z" + h, *p), w=keys("y" + h, *p))
         else:
-            act("z3" + h, T.z32[:, 4 * a:4 * e], T.zt[:, 4 * a:4 * e], F.Copy, keys("z" + h, 0, 4), "y" + h, scale=32.0)
+            act("z3%s%d" % (h, b), T.z32[:, o], T.zt[:, o], F.Copy, keys("z" + h, *p), keys("y" + h, *p), scale=32.0)
 
     def add(t, h, b):
         a, e = HALF[h]
         k = b + (4 if h == "l" else 0)
-        tt("add%s%d" % (h, b), plane(t + 1, b, a, e), bank(k, e - a), T.z32[:, 4 * a + b:4 * e:4], A.add, "ps%d y%s" % (k, h), "own%d%d%s" % ((t + 1) % 2, b, h))
+        tt("add%s%d" % (h, b), plane(t + 1, b, a, e), bank(k, e - a), T.z32[:, 4 * a + b:4 * e:4], A.add, "ps%d y%s%d" % (k, h, b),
+           "own%d%d%s" % ((t + 1) % 2, b, h))
 
     def state(t, h, b, q):
         a, e = HALF[h]
@@ -392,177 +486,81 @@ def rank_program(g, core, T, topo):
         else:
             act("xs" + h, T.xt[:, 4 * a + b:4 * e:4], plane(t + 1, b, a, e), F.Copy, r, w, scale=0.03125)
 
-    def unpacker(b):
-        a = 516 * (b % 2) + 2 - b // 2 * 2
-        quant("qe", T.ec[:, 128 * b:128 * b + 128], T.es[:, 128 * b:128 * b + 128], T.eb[:, a:a + 512], "eb%d" % (b % 2), "eq%d" % b)
-
     dma("s", "ldu", T.ut[:], T.u[:], w="ut")
     dma("y", "ldxh", T.xt[:, 4 * LO:4 * C], T.x[:, 4 * LO:4 * C], w=keys("xh", 0, 4))
     dma("y", "ldx", T.xt[:, 0:4 * LO], T.x[:, 0:4 * LO], w=keys("xl", 0, 4))
     iota("gi0", T.pi[:, 0:1], [[1, 1]], 0, 1, "pi0", small=False)
     iota("gi4", T.uli[:], [[1, 2], [16, 8]], 0, 0, "uli", small=False)
     iota("gi1", T.tmp[:], [[0, NB], [1, 16]], 0, 0, "tmp")
+    for k0, n, w, p in PAIRS.values():
+        for a, step, c in ((0, w, BASE), (16 * k0 + 18, w + 16, BASE), (16 * k0 + 17, w + 16, -SHIFT), (w - 1, w, -SHIFT)):
+            iota("gi3", T.cmp[:, p + a:p + w * n:step], [[0, n]], int(c), 0, "cmpx" if k0 and a == w - 1 else "cmpx%d" % (p + a))
     iota("gi2", T.iot[:, 0:C], [[1, C]], 0, 0, "iot")
-    iota("gi3", T.one[:], [[0, 516]], 1, 0, "one")
     third = TOT // 3
-    fill("fill", T.dl[:, 0:third], 1.5, "dl0")
+    fill("n2", T.dl[:, 0:third], 1.5, "dl0")
     ts("q0", T.pi[:, 1:2], T.pi[:, 0:1], 15, A.bitwise_and, r="pi0", w="pi1")
     fill("fill", T.dl[:, third:2 * third], 1.5, "dl1")
     cp("q1", col(0), T.pi[:, 1:2], "pi1", "c0")
-    cp("ul", T.ul[:], T.uli[:], "uli", "ul")
+    cp("q0", T.ul[:], T.uli[:], "uli", "ul")
     fill("fill", T.dl[:, 2 * third:TOT], 1.5, "dl2")
     fill("pat", T.pat[:, 0:1], -BASE, "pat0")
     fill("pat", T.pat[:, 1:2], PARK, "pat1")
     ts("hot", T.hot[:], T.tmp[:], col(0), A.is_equal, -1.0, A.mult, "tmp c0", "hot")
-    lin("qs", col(1), col(0), 1.0, 0.5, "c0", "c1")
-    lin("qs", col(2), col(0), -1.0, 0.5, "c0", "c2")
+    lin("mx", T.one[:], T.dl[:, 0:516], 0.0, 1.0, "dl0", "one")
     act("qs", col(4), col(0), F.Relu, "c0", "c4", bias=-14.0)
-    lin("mx", T.cap[:], T.tmp[:], 0.0, float(CAP), "tmp", "cap")
-    act("ca", T.ca[:], T.tmp[:], F.Sign, "tmp c1", "ca", scale=-1.0, bias=col(1))
-    act("ca", T.cb[:], T.tmp[:], F.Sign, "tmp c2", "cb", bias=col(2))
+    lin("qs", col(9), col(0), 1024.0, -15360.0, "c0", "c9")
+    lin("qs", col(8), col(4), 1.0, -1.0, "c4", "c8")
+    lin("qs", col(6), col(4), -WIPE, 0.75 * U, "c4", "c6")
     quant("qu", T.uc[:], T.us[:], T.ut[:], "ut", "uq")
     ts("pat", T.pat[:, 2:18], T.hot[:, 15::-1], PARK, A.mult, 1.5, A.add, "hot", "pat2")
-    ts("keep", T.keep[:], T.tmp[:, 0:C - LO], col(0), A.not_equal, r="tmp c0", w="keep")
+    ts("n16", T.keep[:], T.tmp[:, 0:C - LO], col(0), A.not_equal, r="tmp c0", w="keep")
     pick(0)
-    ts("keep", T.hop[:], T.tmp[:, 0:LO], col(0), A.is_equal, r="tmp c0", w="hop")
+    quant_x(0, "h")
+    signed("h")
+    pick(1)
+    score(0, "sh", 0, 0, LO, C)
     for k in range(NB):
         a = 0 if k else 1
         act("kz", T.dl[:, _start(k) - 1 + a:_start(k) + 17], T.pat[:, a:18], F.Copy, "pat0 pat1 pat2 dl0 dl1 dl2", "dk%d" % k)
     act("kz", T.dl[:, TOT - 1:TOT], T.pat[:, 0:1], F.Copy, "pat0 dl2", "dk")
-    quant_x(0, "h")
-    for k0, n, w, p in PAIRS.values():
-        for a, step, c in ((0, w, BASE), (16 * k0 + 18, w + 16, BASE), (16 * k0 + 17, w + 16, -SHIFT), (w - 1, w, -SHIFT)):
-            fill("q4", T.cmp[:, p + a:p + w * n:step], c, "cmpx" if k0 and a == w - 1 else "cmpx%d" % (p + a))
-    score(0, "sh", 0, 0, LO, C)
     quant_x(0, "l")
-    pick(1)
     mask("h")
+    signed("l")
+    fill("q1", T.cum[:, 0:1], 0.0, "cum0")
 
     for t in range(3):
-        lm = T["lm%d" % t]
         nbulk = send_state(t, False)
         if t == 0:
             unit(0)
-        score(t, "sa", 4, 0, 0, LO)
+        score(t, "sa", 4, 0, 0, LO + 16 * MINE["h"])
         score(t, "sb", 1, 0, 0, C)
         score(t, "s1", 2, 1, 0, C)
-        hold("h")
-        mask("l")
-        for j in range(5):
-            compare(NB - 1 - j, "sg%d" % j)
-            compare(KV + j, "sg%d" % j)
-        if t == 0:
-            fill("q2", T.cum[:, 0:1], 0.0, "cum0")
-            lin("mx", T.mx[:], T.hot[:], 8320.0, 128.0, "hot", "mx")
-        hold("l")
-        ts("wt", T.wt[:], bank(2), 0.0, A.is_gt, r="ps2", w="wt")
-        for k in range(KV):
-            compare(k)
-        count("h", 0, 2)
-        count("l", 0, 4)
-        for j in range(2, 5):
-            count("h", j, j + 1)
-        table(t, "l", "s")
-        scan("cum", T.cum[:, 1:C + 1], T.wt[:], T.cap[:], 0.0, A.add, A.min, "wt cap", "cum")
-        table(t, "h", "v")
-        ntab = send_table(t)
-        send_state(t, True)
-        if t == 0:
-            unit(1)
-            lin("qs", col(7), col(4), 1.0, -WIPE - 1.0, "c4", "c7")
-            for a in (0, C):
-                lin("taba", T.taba[:, a:a + C], T.iot[:, 0:C], -2 * U, 289.25 * U, "iot", "taba" if a else "taba0")
-        scan("e1", T.e1[:], T.mx[:], T.cum[:, 1:C + 1], 0.0, A.add, A.max, "mx cum", "e1")
-        scan("e1", T.e2[:], T.mx[:], T.cum[:, 0:C], 0.0, A.add, A.max, "mx cum cum0", "e2")
-        lin("p2", T.p2[:], lm[:, 0:NB], 1.0, float(C), "lm%dl0 lm%dl1 lm%dh0 lm%dh1" % (t, t, t, t), "p2")
-        if t == 0:
-            lin("qs", T.iod[:], T.iot[:, 0:C:16], 1.0, col(0), "iot c0", "iod")
-            lin("cs2", T.ca[:, 15:C:16], T.iot[:, 0:NB], 0.0, WIPE, "iot", "ca")
-            lin("cs2", T.cb[:, 15:C:16], T.iot[:, 0:NB], 0.0, col(7), "iot c7", "cb")
-            for a in (0, C):
-                lin("tabb", T.tabb[:, a:a + C], T.iot[:, 0:C], 2 * U, -288.5 * U, "iot", "tabb" if a else "tabb0")
-            lin("qs", col(8), col(4), -1.0, 1.0, "c4", "c8")
-            lin("qs", col(6), col(4), 1.0, TOP - 1.0, "c4", "c6")
-            fill("q2", T.a16[:, C:C + 1], -TOP, "a16e0")
-            fill("q2", T.b16[:, C:C + 1], 0.0, "a16e")
-        tt("own", T.own[:], T.e1[:, 15:C:16], T.e2[:, 15:C:16], A.is_equal, "e1 e2", "own")
-        if t == 2:
-            quant("qu", T.vc[:], T.vs[:], T.vt[:], "vt", "vq")
-        tt("p3", T.p3[:], T.p2[:], T.own[:], A.mult, "own p2", "p3")
-        lin("n1", T.n1[:], T.own[:], -float(C), float(C), "own", "n1")
-        tt("mm", T.mm[:], T["tl%d" % t][:], T.p3[:], A.max, "p3", "mm", ext=[("tab%d" % t, ntab)])
-        if t == 0:
-            dma("y", "ldw", T.wq[:].bitcast(u8), T.wc[:], "mm", "wq")
-            dma("y", "ldw", T.wp[:], T.ws[:], "", "wp")
-            unpacker(0)
-        if t == 1:
-            dma("y", "ldu", T.vt[:], T.v[:], "mm", "vt")
-        cp("m16", T.m16[:], T.mm[:], "mm", "m16")
-        tt("n2", T.n2[:], T.n1[:], T.iod[:], A.add, "n1 iod", "n2")
-        addends("h")
-        addends("l")
-        last("h")
-        last("l")
-        ad("h")
-        cp("n16", T.n16[:], T.n2[:], "n2", "n16")
-        if t == 0:
-            lin("taba", T.iot[:, C:2 * C], T.iot[:, 0:C], 1.0, float(C), "iot", "iot2")
-            lin("mx", T.mo[:], T.hot[:], 66560.0, 1024.0, "hot", "mo")
-        act("name", T.name[:], T.iot[:].indirect(T.n16[:]), F.Copy, "iot iot2 n16", "name")
-        if t == 0:
-            lin("mx", col(9), col(0), 1024.0, -15360.0, "c0", "c9")
-            for b in range(4):
-                act("kz", plane(0, b, 0, C), T.xt[:, b:4 * C:4], F.Copy, "xl%d xh%d" % (b, b), "own0%dl own0%dh" % (b, b), scale=32.0)
-        bd("h")
-        ad("l")
-        runs("h")
-        bd("l")
-        v1("h")
-        if t == 0:
-            unpacker(1)
-        runs("l")
-        v2("h")
-        b16("h")
-        v1("l")
-        if t == 0:
-            unpacker(2)
-            unpacker(3)
-        for k in range(NB - 2, KV - 1, -1):
-            push(k)
-            if k == NB - 3:
-                v2("l")
-            if k == NB - 4:
-                b16("l")
-        for k in range(KV - 1, -1, -1):
-            push(k)
-            if k == KV - 3:
-                places("h")
-        for b, k in enumerate((3, 5, 6, 7)):
-            mm("d%d" % b, k, T.ec[:, 128 * b:128 * b + 128], T.es[:, 128 * b:128 * b + 128], T["lc%d" % t][:], T["ls%d" % t][:],
-               "eq%d" % b, ext=[("bulk%d" % t, nbulk)] if b == 0 else [])
-            act("dev", plane(t, b, C), bank(k), F.Copy, "ps%d" % k, "far%d" % b, scale=32.0)
-        scatter("h")
-        places("l")
-        scatter("l")
-        oext("h")
-        oext("l")
-        olist("h")
-        olist("l")
+        step = {"mask": mask, "hold": hold, "compare": compare, "count": count, "wanted": wanted, "sums": sums, "counted": counted,
+                "owned": owned, "kept": kept, "n1": n1, "n2": n2, "n16": n16, "name": name, "m16": m16, "addends": addends,
+                "last": last, "ad": ad, "runs": runs, "v1": v1, "v2": v2, "a16": a16, "push": push, "places": places,
+                "scatter": scatter, "oext": oext, "olist": olist,
+                "table": lambda h, q: table(t, h, q), "send": lambda h: send(t, h), "shifted": lambda h: shifted(t, h),
+                "mix": lambda h: mix(t, h), "loads": lambda: loads(t), "unpack": lambda: unpack(t, nbulk),
+                "once": lambda i: t == 0 and once(i), "unpacker": lambda b: t == 0 and unpacker(b),
+                "vtile": lambda: t == 2 and quant("qu", T.vc[:], T.vs[:], T.vt[:], "vt", "vq")}
+        for w in ORDER:
+            n, *arg = w.split(".")
+            step[n](*[int(x) if x.isdigit() else x for x in arg])
         if t == 2:
             dma("y", "sto", T.od[:], T.orow[0:128:16, :], "orow")
         for w in LAYER:
-            step, h = w[0], w[1]
-            if step == "g":
+            n, h = w[0], w[1]
+            if n == "g":
                 gather(t, h, int(w[2]), w[3])
-            elif step == "q":
+            elif n == "q":
                 quant_z(h)
-            elif step == "z":
-                z32(h, w[2])
-            elif step == "a":
+            elif n == "z":
+                z32(h, int(w[2]), w[3])
+            elif n == "a":
                 add(t, h, int(w[2]))
-            elif step == "x":
+            elif n == "x":
                 state(t, h, int(w[2]), w[3])
-            elif step == "Q":
+            elif n == "Q":
                 quant_x(t + 1, h)
                 if h == "h" and t < 2:
                     score(t + 1, "sh", 0, 0, LO, C)

from concourse.mybir import dt, AluOpType, ActivationFunctionType

C, CAP, NB = 288, 128, 18
MASKS = [1, 2, 4]
KV = 8
LO = 16 * KV
HALF = {"h": (LO, C), "l": (0, LO)}
MINE = {"h": 3, "l": 2}
PAIRS = {"l": (0, KV // 2, 16 * (KV + 1) + 4, 0), "h": (KV, (NB - KV) // 2, 16 * (NB + KV + 1) + 4, (16 * (KV + 1) + 4) * KV // 2)}
TOT = PAIRS["h"][3] + PAIRS["h"][1] * PAIRS["h"][2]
ORDER = """hold.h compare.17.16 mask.l compare.8.9.10 compare.15 compare.14.11 wanted hold.l count.h.0.2 count.h.2.3 sums compare.13.12
count.h.3.4 count.h.4.5 compare.7.6.5.4.3.2 compare.0.1 once.0 unpacker.0 table.h.v send.h once.1 shifted.h count.l.0.4 counted
table.l.s send.l once.2 unpacker.2 vtile owned kept.h mix.h shifted.l m16.h n1 once.3 kept.l ad.h n2 addends.h mix.l runs.h m16.l
unpacker.1 last.h v1.h ad.l addends.l v2.h last.l a16.h n16 once.4 runs.l name push.14.17 loads once.5 v1.l unpacker.3 push.8.11
v2.l a16.l unpack push.11.14 push.5.8 places.8.18 push.0.5 scatter.8.18 places.0.8 scatter.0.8 oext.h oext.l olist.h olist.l""".split()
LAYER = ("gh0v gh2s gh1v gh3s gl0v gl2s gl3s qh gl1v zh0v zh1v zh2s zh3s ql zl4s ah0 xh0s ah1 xh1s ah2 xh2s ah3 xh3s "
         "al0 al1 al2 al3 xl0s xl1s xl2s Qh xl3v Ql mh").split()
U = 2.0 ** -10
TOP = 2.0 ** 14
WIPE = 1.5 * 2.0 ** 23
BASE = 2.0 ** 23
PARK = 2.0 ** 40
SHIFT = 64.0
OW = C - 16 + 1


def _start(k):
    k0, n, w, p = PAIRS["l" if k < KV else "h"]
    j = k - k0
    return p + (w * j if j < n else (w + 16) * (2 * n - 1 - j) + 16 * k0 + 18)


def _lst(h):
    return slice(HALF[h][0] // 16, HALF[h][1] // 16)


F32, BF, F16, U16, I32, Q4, U8 = "float32", "bfloat16", "float16", "uint16", "int32", "float8_e4m3fn_x4", "uint8"


def _sb(n, t):
    return ("sbuf", [128, n], t)


SCRATCH = {
    "ps": ("psum", [128, 4096], F32),
    "xt": _sb(4 * C, BF), "ut": _sb(512, BF), "vt": _sb(512, BF), "zt": _sb(4 * C, BF), "z32": _sb(4 * C, BF),
    "win0": _sb(8 * C, BF), "win1": _sb(8 * C, BF),
    "uc": _sb(128, Q4), "us": _sb(128, U8), "upc": _sb(256, Q4), "ups": _sb(256, U8),
    "vc": _sb(128, Q4), "vs": _sb(128, U8), "ec": _sb(512, Q4), "es": _sb(512, U8),
    "wq": _sb(512, Q4), "wp": _sb(512, U8), "zc": _sb(C, Q4), "zs": _sb(C, U8),
    "eb": _sb(1032, BF),
    "uli": _sb(16, I32), "ul": _sb(16, U16), "pi": _sb(2, I32), "cc": _sb(16, F32),
    "iot": _sb(2 * C, F32), "tmp": _sb(C, BF), "hot": _sb(C, BF), "hop": _sb(C, BF), "keep": _sb(C - LO, BF),
    "mx": _sb(C, BF), "mo": _sb(C, F32), "one": _sb(516, BF), "iod": _sb(NB, F32),
    "taba": _sb(2 * C, F32), "tabb": _sb(2 * C, F32), "ca": _sb(C, BF),
    "sm": _sb(C, F32), "hs": _sb(C, F32), "cmp": _sb(TOT, BF), "cs": _sb(TOT, BF), "dl": _sb(TOT, BF), "pat": _sb(18, BF),
    "wt": _sb(C, F16), "cum": _sb(C + 2, F16), "e1": _sb(C, F16), "e2": _sb(C, F16),
    "own": _sb(NB, F32), "n1": _sb(NB, F32), "n2": _sb(NB, F32), "n16": _sb(NB, U16), "name": _sb(C, F32),
    "p2": _sb(NB, F32), "p3": _sb(NB, F32),
    "mm": _sb(NB, F32), "m16": _sb(NB, U16),
    "b32": _sb(C, F32), "ad": _sb(C, F32), "dout": _sb(C, F32),
    "al": _sb(NB, F32), "v1": _sb(NB, F32), "v2": _sb(NB, F32),
    "a16": _sb(C + 2, F16), "b16": _sb(C + 2, F16), "o16": _sb((NB - 1) * OW, F16), "pl": _sb(NB, U16),
    "orow": _sb(C, F32), "oext": _sb(C, F32), "ol": _sb(NB, U16), "ysb": _sb(C, F32),
    "rt": _sb(NB, F32),
}
for _t in range(4):
    SCRATCH["xc%d" % _t] = _sb(C, Q4)
    SCRATCH["xs%d" % _t] = _sb(C, U8)
for _t in range(3):
    SCRATCH["lc%d" % _t] = _sb(C, Q4)
    SCRATCH["ls%d" % _t] = _sb(C, U8)
    SCRATCH["rc%d" % _t] = _sb(C, Q4)
    SCRATCH["rs%d" % _t] = _sb(C, U8)
    SCRATCH["lm%d" % _t] = _sb(NB + 2, F32)
    SCRATCH["tl%d" % _t] = _sb(NB, F32)

LOCAL = ["s%d" % _t for _t in range(133)]
SEMAPHORES = LOCAL + ["out", "hc", "hd", "hth", "htl"] + ["%s%d" % (n, t) for n in ("bulk", "tabh", "tabl", "hsc") for t in range(3)]


def _helpers(topo, T, r):
    c = T.cores[r]
    return [h for h in topo.cores_of(c) if T.rank_of(h) is None and topo.die(h) == topo.die(c)
            and all(topo.may_write(h, T.cores[r ^ m]) for m in MASKS)][:2]


def _write(g, T, topo, src, dst, out, in_, sem):
    rid, pid = topo.addr(dst, src)
    g.remote_dma(out, in_, T.sem[sem], T.sem.out, pid, rid, topo.mask(src, dst))
    return len(topo.engines(src, dst))


def _helper_program(g, core, T, topo, r, i):
    own, sent = T.cores[r], 0
    n = len(topo.engines(own, core))
    u8 = dt.uint8
    for t, m in enumerate(MASKS):
        far = T.cores[r ^ m]
        near, hop = far in topo.cores_of(own), not topo.may_write(own, far)
        lc, rc = T["lc%d" % t], T["rc%d" % t]
        if i == 0 and (near or hop):
            g.wait_ge(T.sem["hsc%d" % t], n)
            sent += _write(g, T, topo, core, far, T["ls%d" % t][:], T["rs%d" % t][:], "bulk%d" % t)
        if i == 0 and hop:
            for h in "hl":
                g.wait_ge(T.sem["ht" + h], n)
                sent += _write(g, T, topo, core, far, T["tl%d" % t][:, _lst(h)], T.rt[:, _lst(h)], "tab%s%d" % (h, t))
            g.wait_ge(T.sem.hd, n)
            sent += _write(g, T, topo, core, far, lc[:, 0:LO].bitcast(u8), rc[:, 0:LO].bitcast(u8), "bulk%d" % t)
        if i == 1 and hop:
            g.wait_ge(T.sem.hc, n)
            sent += _write(g, T, topo, core, far, lc[:, LO:C].bitcast(u8), rc[:, LO:C].bitcast(u8), "bulk%d" % t)
    g.wait_ge(T.sem.out, sent)


def _emit(g, T, ops):
    queue = {"g": g, "v": g.vector, "s": g.scalar, "t": g.tensor, "y": g.sync}
    know = {k: 0 for k in queue}
    sem, count, members, waited = {}, {}, {}, {}
    writer, readers = {}, {}
    for n, o in enumerate(ops):
        q, need = o["q"], set()
        for k in o["r"] + o["w"]:
            if k in writer:
                need.add(writer[k])
        for k in o["w"]:
            need.update(readers.get(k, []))
        for d in sorted(need, reverse=True):
            if know[q] >> d & 1:
                continue
            lab = ops[d]["label"]
            queue[q].wait_ge(sem[lab], count[lab])
            waited[lab] = count[lab]
            for e in members[lab]:
                know[q] |= ops[e]["know"] | 1 << e
        for s, v in o["ext"]:
            queue[q].wait_ge(T.sem[s], v)
        o["know"] = know[q]
        ins = o["fn"](queue[q])
        lab = o["label"]
        if lab is None:
            continue
        if lab not in sem:
            sem[lab] = T.sem[LOCAL[len(sem)]]
        ins.then_inc(sem[lab], o["inc"])
        count[lab] = count.get(lab, 0) + o["inc"]
        members.setdefault(lab, []).append(n)
        for k in o["r"]:
            readers.setdefault(k, []).append(n)
        for k in o["w"]:
            writer[k], readers[k] = n, []
    for lab in count:
        if waited.get(lab, 0) < count[lab]:
            g.wait_ge(sem[lab], count[lab])


def rank_program(g, core, T, topo):
    rank = T.rank_of(core)
    if rank is None:
        for r in range(len(T.cores)):
            hs = _helpers(topo, T, r)
            if core in hs:
                _helper_program(g, core, T, topo, r, hs.index(core))
        return
    A, F = AluOpType, ActivationFunctionType
    ops, sent = [], [0]
    helpers = _helpers(topo, T, rank)

    def op(q, label, fn, r="", w="", ext=(), inc=1):
        ops.append({"q": q, "label": label, "fn": fn, "r": r.split(), "w": w.split(), "ext": list(ext), "inc": inc})

    def ts(label, out, in0, s1, o0, s2=None, o1=None, r="", w=""):
        if o1 is None:
            op("v", label, lambda e: e.tensor_scalar(out, in0, s1, None, o0), r, w)
        else:
            op("v", label, lambda e: e.tensor_scalar(out, in0, s1, s2, o0, o1), r, w)

    def tt(label, out, a, b, o, r="", w="", ext=()):
        op("v", label, lambda e: e.tensor_tensor(out, a, b, o), r, w, ext)

    def cp(label, out, a, r="", w=""):
        op("v", label, lambda e: e.tensor_copy(out, a), r, w)

    def scan(label, out, a, b, init, o0, o1, r="", w=""):
        op("v", label, lambda e: e.tensor_tensor_scan(out, a, b, init, o0, o1), r, w)

    def fill(label, ap, c, w):
        op("v", label, lambda e: e.memset(ap, c), "", w)

    def act(label, out, a, f, r="", w="", **kw):
        op("s", label, lambda e: e.activation(out, a, f, **kw), r, w)

    def lin(label, out, a, scale, bias, r, w):
        act(label, out, a, F.Identity, r, w, scale=scale, bias=bias)

    def quant(label, c, s, a, r, w):
        op("v", label, lambda e: e.quantize_mx(c, s, a), r, w)

    def mm(label, b, lc, ls, rc, rs, r, ext=(), n=C):
        op("t", label, lambda e: e.matmul_mx(bank(b, n), lc, ls, rc, rs, True, True), r, "ps%d" % b, ext)

    def dma(q, label, out, a, r="", w=""):
        op(q, label, lambda e: e.dma_start(out, a), r, w, inc=16)

    def iota(label, out, pattern, base, cm, w, small=True):
        if small:
            op("g", label, lambda e: e.iota(out, pattern, base, cm, allow_small_or_imprecise_dtypes=True), "", w)
        else:
            op("g", label, lambda e: e.iota(out, pattern, base, cm), "", w)

    def bank(b, n=C):
        return T.ps[:, 512 * b:512 * b + n]

    def col(j):
        return T.cc[:, j:j + 1]

    def write(dst, out, a, sem, r):
        def fn(e):
            sent[0] += _write(e, T, topo, core, dst, out, a, sem)
        op("g", None, fn, r)

    def keys(name, a, b):
        return " ".join("%s%d" % (name, k) for k in range(a, b))

    u8 = dt.uint8

    def send_state(t, late):
        far = T.cores[rank ^ MASKS[t]]
        xc, xs, lo, hi = T["xc%d" % t], T["xs%d" % t], "xq%dl" % t, "xq%dh" % t
        lc, rc = T["lc%d" % t], T["rc%d" % t]
        theirs = [len(topo.engines(h, core)) for h in _helpers(topo, T, rank ^ MASKS[t])]
        if far in topo.cores_of(core):
            if not late:
                write(helpers[0], T["rs%d" % t][:], xs[:], "hsc%d" % t, lo + " " + hi)
                write(far, lc[:].bitcast(u8), xc[:].bitcast(u8), "bulk%d" % t, lo + " " + hi)
            return len(topo.engines(far, core)) + theirs[0]
        if not topo.may_write(core, far):
            if not late:
                write(helpers[1], rc[:, LO:C].bitcast(u8), xc[:, LO:C].bitcast(u8), "hc", hi)
                write(helpers[0], T["rs%d" % t][:], xs[:], "hsc%d" % t, lo + " " + hi)
                write(helpers[0], rc[:, 0:LO].bitcast(u8), xc[:, 0:LO].bitcast(u8), "hd", lo)
            return 2 * theirs[0] + theirs[1]
        if not late:
            write(far, lc[:, LO:C].bitcast(u8), xc[:, LO:C].bitcast(u8), "bulk%d" % t, hi)
        else:
            write(far, lc[:, 0:LO].bitcast(u8), xc[:, 0:LO].bitcast(u8), "bulk%d" % t, lo)
            write(far, T["ls%d" % t][:], xs[:], "bulk%d" % t, lo + " " + hi)
        return 3 * len(topo.engines(far, core))

    def send(t, h):
        far, lm, key = T.cores[rank ^ MASKS[t]], T["lm%d" % t][:, _lst(h)], keys("lm%d%s" % (t, h), 0, 2)
        if topo.may_write(core, far):
            write(far, T["tl%d" % t][:, _lst(h)], lm, "tab%s%d" % (h, t), key)
        else:
            write(helpers[0], T.rt[:, _lst(h)], lm, "ht" + h, key)
        if h == "l":
            send_state(t, True)
            if t == 0:
                unit(1)

    def loads(t):
        if t == 0:
            dma("y", "ldw", T.wq[:].bitcast(u8), T.wc[:], "mml", "wq")
            dma("y", "ldw", T.wp[:], T.ws[:], "", "wp")
        if t == 1:
            dma("y", "ldu", T.vt[:], T.v[:], "mml", "vt")

    def unit(i):
        op("g", "gi%d" % i, lambda e: e.affine_select(T.eb[:, 516 * i:516 * i + 516], T.one[:], [[1, 516]], A.is_equal, 0.0, -2 - i, -4), "one", "eb%d" % i)

    def unpacker(b):
        a = 516 * (b % 2) + 2 - b // 2 * 2
        quant("qe", T.ec[:, 128 * b:128 * b + 128], T.es[:, 128 * b:128 * b + 128], T.eb[:, a:a + 512], "eb%d" % (b % 2), "eq%d" % b)

    def pick(a):
        o, i = slice(128 * a, 128 * a + 128), T.ul[:, 8 * a:8 * a + 8]
        cp("pc%d" % a, T.upc[:, o].bitcast(dt.uint32), T.uc[:].bitcast(dt.uint32).indirect(i), "uq ul", "upc%d" % a)
        act("pz%d" % a, T.ups[:, o], T.us[:].indirect(i), F.Copy, "uq ul", "ups%d" % a)

    def signed(h):
        a, e = HALF[h]
        c = a + 16 * MINE[h]
        ts("hop", T.hop[:, a:c], T.tmp[:, a:c], col(0), A.is_equal, r="tmp c0", w="hop" + h)
        ts("hop", T.hop[:, c:e], T.tmp[:, c:e], col(0), A.is_equal, -1.0, A.mult, "tmp c0", "hoq" + h)

    def once(i):
        if i == 0:
            lin("mx", T.mx[:], T.hot[:], 65.0, 1.0, "hot", "mx")
        if i == 1:
            for a in (0, C):
                lin("taba", T.taba[:, a:a + C], T.iot[:, 0:C], -2 * U, 289.25 * U, "iot", "taba" if a else "taba0")
            lin("ca", T.ca[:], T.hot[:], WIPE, 0.0, "hot", "ca")
        if i == 2:
            lin("ca", T.ca[:, 15:C:16], T.hot[:, 15:C:16], WIPE, WIPE, "hot", "ca")
            for a in (0, C):
                lin("tabb", T.tabb[:, a:a + C], T.iot[:, 0:C], 2 * U, -288.5 * U, "iot", "tabb" if a else "tabb0")
            lin("qs", T.iod[:], T.iot[:, 0:C:16], 1.0, col(0), "iot c0", "iod")
        if i == 3:
            fill("q1", T.a16[:, C:C + 1], -TOP, "a16e0")
            fill("q1", T.b16[:, C:C + 1], 0.0, "a16e")
        if i == 4:
            lin("taba", T.iot[:, C:2 * C], T.iot[:, 0:C], 1.0, float(C), "iot", "iot2")
            lin("mx", T.mo[:], T.hot[:], 66560.0, 1024.0, "hot", "mo")
        if i == 5:
            for b in range(4):
                act("kz", plane(0, b, 0, C), T.xt[:, b:4 * C:4], F.Copy, "xl%d xh%d" % (b, b), "own0%dl own0%dh" % (b, b), scale=32.0)

    def quant_x(t, h):
        a, e = HALF[h]
        quant("qx" + h, T["xc%d" % t][:, a:e], T["xs%d" % t][:, a:e], T.xt[:, 4 * a:4 * e], keys("x" + h, 0, 4), "xq%d%s" % (t, h))

    def score(t, label, b, side, a, e):
        o = slice(128 * side, 128 * side + 128)
        r = "upc%d ups%d" % (side, side) + (" xq%dl" % t if a < LO else "") + (" xq%dh" % t if e > LO else "")
        mm(label, b, T.upc[:, o], T.ups[:, o], T["xc%d" % t][:, a:e], T["xs%d" % t][:, a:e], r, n=e - a)

    def mask(h):
        a, e = HALF[h]
        b = 0 if h == "h" else 4
        tt("sm" + h, T.sm[:, a:e], bank(b, e - a), T.hop[:, a:e], A.mult, "ps%d hop%s hoq%s" % (b, h, h), "sm" + h)

    def hold(h):
        a, e = HALF[h]
        scan("hs" + h, T.hs[:, a:e], T.keep[:, 0:e - a], T.sm[:, a:e], 0.0, A.mult, A.add, "keep sm" + h, "hs" + h)

    def compare(*ks):
        for k in ks:
            n, p, h = 16 * (k + 1), _start(k) + 1, "l" if k < KV else "h"
            if k - PAIRS[h][0] < MINE[h]:
                ts("cmp%d" % ks[0], T.cmp[:, p:p + n], T.ps[:, 2048 + n - 1:2047:-1], T.hs[:, n - 1:n], A.is_lt, -1.0, A.mult, "ps4 hs" + h, "cmp%d" % k)
            else:
                act("cmp%d" % ks[0], T.cmp[:, p:p + n], T.ps[:, 512 + n - 1:511:-1], F.Sign, "ps1 hs" + h, "cmp%d" % k, bias=T.hs[:, n - 1:n])

    def count(h, a, b):
        k0, n, w, p = PAIRS[h]
        p, q = p + w * a, p + w * b
        scan("cs" + h, T.cs[:, p:q], T.cmp[:, p:q], T.dl[:, p:q], 0.0, A.add, A.add,
             keys("cmp", k0 + a, k0 + b) + " " + keys("cmp", k0 + 2 * n - b, k0 + 2 * n - a) + " dk cmpx", "cs%s%d" % (h, a))

    def table(t, h, q):
        k0, n, w, p = PAIRS[h]
        lm, r = T["lm%d" % t], keys("cs" + h, 0, n)
        for i, (o, a) in enumerate(((lm[:, k0:k0 + n], T.cs[:, p + 16 * k0 + 17:p + w * n:w + 16]),
                                    (lm[:, k0 + n:k0 + 2 * n], T.cs[:, p + w * n - 1:p:-w]))):
            if q == "v":
                ts("lm" + h, o, a, SHIFT, A.add, 0.5, A.mult, r, "lm%d%s%d" % (t, h, i))
            else:
                lin("lm" + h, o, a, 0.5, SHIFT / 2, r, "lm%d%s%d" % (t, h, i))

    def wanted():
        ts("wt", T.wt[:], bank(2), 0.0, A.is_gt, 1.0 / CAP, A.mult, "ps2", "wt")

    def sums():
        scan("cum", T.cum[:, 1:C + 1], T.wt[:], T.one[:, 0:C], 0.0, A.add, A.min, "wt one", "cum")

    def counted():
        scan("e1", T.e1[:], T.mx[:], T.cum[:, 1:C + 1], 0.0, A.add, A.max, "mx cum", "e1")
        scan("e1", T.e2[:], T.mx[:], T.cum[:, 0:C], 0.0, A.add, A.max, "mx cum cum0", "e2")

    def owned():
        tt("own", T.own[:], T.e1[:, 15:C:16], T.e2[:, 15:C:16], A.is_equal, "e1 e2", "own")

    def shifted(t, h):
        lin("p2" + h, T.p2[:, _lst(h)], T["lm%d" % t][:, _lst(h)], 1.0, float(C), keys("lm%d%s" % (t, h), 0, 2), "p2" + h)

    def kept(h):
        tt("p3" + h, T.p3[:, _lst(h)], T.p2[:, _lst(h)], T.own[:, _lst(h)], A.mult, "own p2" + h, "p3" + h)

    def n1():
        lin("n1", T.n1[:], T.own[:], -float(C), float(C), "own", "n1")

    def n2():
        tt("n2", T.n2[:], T.n1[:], T.iod[:], A.add, "n1 iod", "n2")

    def n16():
        cp("n16", T.n16[:], T.n2[:], "n2", "n16")

    def name():
        act("name", T.name[:], T.iot[:].indirect(T.n16[:]), F.Copy, "iot iot2 n16", "name")

    def mix(t, h):
        far = T.cores[rank ^ MASKS[t]]
        n = len(topo.engines(far if topo.may_write(far, core) else _helpers(topo, T, rank ^ MASKS[t])[0], core))
        tt("mm" + h, T.mm[:, _lst(h)], T["tl%d" % t][:, _lst(h)], T.p3[:, _lst(h)], A.max, "p3" + h, "mm" + h, ext=[("tab%s%d" % (h, t), n)])

    def m16(h):
        cp("m16" + h, T.m16[:, _lst(h)], T.mm[:, _lst(h)], "mm" + h, "m16" + h)

    def addends(h):
        a, e = HALF[h]
        act("b32" + h, T.b32[:, a:e], T.tabb[:].indirect(T.m16[:, _lst(h)]), F.Copy, "tabb m16" + h, "b32" + h)
        op("g", "b16" + h, lambda g_: g_.affine_select(T.b16[:, a:e], T.b32[:, a:e], [[0, e - a]], A.is_gt, 0.0, 1, 0), "b32" + h, "b16" + h)

    def last(h):
        a, e = HALF[h]
        lin("al" + h, T.al[:, _lst(h)], T.b32[:, a + 15:e:16], col(8), col(6), "c6 c8 b32" + h, "al" + h)

    def ad(h):
        a, e = HALF[h]
        tt("ad" + h, T.ad[:, a:e], T.taba[:].indirect(T.m16[:, _lst(h)]), T.ca[:, a:e], A.add, "taba ca m16" + h, "ad" + h)

    def runs(h):
        a, e = HALF[h]
        scan("dout" + h, T.dout[:, a:e - 1], T.ad[:, a:e - 1], T.b32[:, a:e - 1], TOP + WIPE, A.add, A.add, "ad%s b32%s" % (h, h), "dout" + h)

    def v1(h):
        a, e = HALF[h]
        tt("v1" + h, T.v1[:, _lst(h)], T.dout[:, a + 14:e:16], T.al[:, _lst(h)], A.add, "dout%s al%s" % (h, h), "v1" + h)

    def v2(h):
        a, e = HALF[h]
        tt("v2" + h, T.v2[:, _lst(h)], T.v1[:, _lst(h)], T.b32[:, a + 15:e:16], A.add, "v1%s b32%s" % (h, h), "v2" + h)

    def a16(h):
        a, e = HALF[h]
        ts("a16" + h, T.a16[:, a:e], T.b16[:, a:e], -1.0, A.mult, 0.75 * U, A.add, "b16" + h, "a16" + h)

    def push(k0, k1):
        for k in range(k1 - 1, k0 - 1, -1):
            a = 16 * k + 16
            scan("scanl" if k < KV else "scanh", T.o16[:, OW * k + 16 * k:OW * k + OW], T.a16[:, a:C + 1], T.b16[:, a:C + 1], T.v2[:, k:k + 1],
                 A.add, A.add, "a16h b16h a16e v2" + ("l" if k < KV else "h") + (" a16l b16l" if a < LO else ""), "o%d" % k)

    def places(a, e):
        if e == NB:
            e -= 1
            ts("pl%d" % a, T.pl[:, e:NB], T.v2[:, e:NB], 0.5 / U, A.mult, C // 2 - TOP * 0.5 / U, A.add, "v2h", "pl%d" % e)
        ts("pl%d" % a, T.pl[:, a:e], T.o16[:, OW * a + OW - 1:OW * e:OW], 0.5 / U, A.mult, float(C // 2), A.add, keys("o", a, e), keys("pl", a, e))

    def scatter(a, e):
        cp("orow", T.orow[:].indirect(T.pl[:, a:e]), T.name[:, 16 * a:16 * e], "name " + keys("pl", a, e), "orow")

    def oext(h):
        a, e = HALF[h]
        scan("oext" + h, T.oext[:, a:e], T.mo[:, a:e], T.orow[:, a:e], 0.0, A.add, A.max, "mo orow", "oext" + h)

    def olist(h):
        a, e = HALF[h]
        ts("ol" + h, T.ol[:, _lst(h)], T.oext[:, a + 15:e:16], col(9), A.add, r="c9 oext" + h, w="ol" + h)

    def plane(t, b, a=0, e=2 * C):
        return T["win%d" % (t % 2)][:, 2 * C * b + a:2 * C * b + e]

    def unpack(t, n):
        for b, k in enumerate((3, 5, 6, 7)):
            mm("d%d" % b, k, T.ec[:, 128 * b:128 * b + 128], T.es[:, 128 * b:128 * b + 128], T["lc%d" % t][:], T["ls%d" % t][:],
               "eq%d" % b, ext=[("bulk%d" % t, n)] if b == 0 else [])
            act("dev", plane(t, b, C), bank(k), F.Copy, "ps%d" % k, "far%d" % b, scale=32.0)

    def gather(t, h, b, q):
        a, e = HALF[h]
        src, out = plane(t, b).indirect(T.ol[:, _lst(h)]), T.zt[:, 4 * a + b:4 * e:4]
        r = "own%d%dl own%d%dh far%d ol%s" % (t % 2, b, t % 2, b, b, h)
        if q == "v":
            ts("zv" + h, out, src, 0.03125, A.mult, r=r, w="z%s%d" % (h, b))
        else:
            act("zs" + h, out, src, F.Copy, r, "z%s%d" % (h, b), scale=0.03125)

    def quant_z(h):
        a, e = HALF[h]
        quant("qz" + h, T.zc[:, a:e], T.zs[:, a:e], T.zt[:, 4 * a:4 * e], keys("z" + h, 0, 4), "zq" + h)
        for b in range(4):
            mm("r%s%d" % (h, b), b + (4 if h == "l" else 0), T.wq[:, 128 * b:128 * b + 128], T.wp[:, 128 * b:128 * b + 128],
               T.zc[:, a:e], T.zs[:, a:e], "wq wp zq" + h, n=e - a)

    def z32(h, b, q):
        a, e = HALF[h]
        o, p = (slice(4 * a + b, 4 * e, 4), (b, b + 1)) if b < 4 else (slice(4 * a, 4 * e), (0, 4))
        if q == "v":
            ts("z3%s%d" % (h, b), T.z32[:, o], T.zt[:, o], 32.0, A.mult, r=keys("z" + h, *p), w=keys("y" + h, *p))
        else:
            act("z3%s%d" % (h, b), T.z32[:, o], T.zt[:, o], F.Copy, keys("z" + h, *p), keys("y" + h, *p), scale=32.0)

    def add(t, h, b):
        a, e = HALF[h]
        k = b + (4 if h == "l" else 0)
        tt("add%s%d" % (h, b), plane(t + 1, b, a, e), bank(k, e - a), T.z32[:, 4 * a + b:4 * e:4], A.add, "ps%d y%s%d" % (k, h, b),
           "own%d%d%s" % ((t + 1) % 2, b, h))

    def state(t, h, b, q):
        a, e = HALF[h]
        r, w = "own%d%d%s" % ((t + 1) % 2, b, h), "x%s%d" % (h, b)
        if q == "v":
            ts("xv" + h, T.xt[:, 4 * a + b:4 * e:4], plane(t + 1, b, a, e), 0.03125, A.mult, r=r, w=w)
        else:
            act("xs" + h, T.xt[:, 4 * a + b:4 * e:4], plane(t + 1, b, a, e), F.Copy, r, w, scale=0.03125)

    dma("s", "ldu", T.ut[:], T.u[:], w="ut")
    dma("y", "ldxh", T.xt[:, 4 * LO:4 * C], T.x[:, 4 * LO:4 * C], w=keys("xh", 0, 4))
    dma("y", "ldx", T.xt[:, 0:4 * LO], T.x[:, 0:4 * LO], w=keys("xl", 0, 4))
    iota("gi0", T.pi[:, 0:1], [[1, 1]], 0, 1, "pi0", small=False)
    iota("gi4", T.uli[:], [[1, 2], [16, 8]], 0, 0, "uli", small=False)
    iota("gi1", T.tmp[:], [[0, NB], [1, 16]], 0, 0, "tmp")
    for k0, n, w, p in PAIRS.values():
        for a, step, c in ((0, w, BASE), (16 * k0 + 18, w + 16, BASE), (16 * k0 + 17, w + 16, -SHIFT), (w - 1, w, -SHIFT)):
            iota("gi3", T.cmp[:, p + a:p + w * n:step], [[0, n]], int(c), 0, "cmpx" if k0 and a == w - 1 else "cmpx%d" % (p + a))
    iota("gi2", T.iot[:, 0:C], [[1, C]], 0, 0, "iot")
    third = TOT // 3
    fill("n2", T.dl[:, 0:third], 1.5, "dl0")
    ts("q0", T.pi[:, 1:2], T.pi[:, 0:1], 15, A.bitwise_and, r="pi0", w="pi1")
    fill("fill", T.dl[:, third:2 * third], 1.5, "dl1")
    cp("q1", col(0), T.pi[:, 1:2], "pi1", "c0")
    cp("q0", T.ul[:], T.uli[:], "uli", "ul")
    fill("fill", T.dl[:, 2 * third:TOT], 1.5, "dl2")
    fill("pat", T.pat[:, 0:1], -BASE, "pat0")
    fill("pat", T.pat[:, 1:2], PARK, "pat1")
    ts("hot", T.hot[:], T.tmp[:], col(0), A.is_equal, -1.0, A.mult, "tmp c0", "hot")
    lin("mx", T.one[:], T.dl[:, 0:516], 0.0, 1.0, "dl0", "one")
    act("qs", col(4), col(0), F.Relu, "c0", "c4", bias=-14.0)
    lin("qs", col(9), col(0), 1024.0, -15360.0, "c0", "c9")
    lin("qs", col(8), col(4), 1.0, -1.0, "c4", "c8")
    lin("qs", col(6), col(4), -WIPE, 0.75 * U, "c4", "c6")
    quant("qu", T.uc[:], T.us[:], T.ut[:], "ut", "uq")
    ts("pat", T.pat[:, 2:18], T.hot[:, 15::-1], PARK, A.mult, 1.5, A.add, "hot", "pat2")
    ts("n16", T.keep[:], T.tmp[:, 0:C - LO], col(0), A.not_equal, r="tmp c0", w="keep")
    pick(0)
    quant_x(0, "h")
    signed("h")
    pick(1)
    score(0, "sh", 0, 0, LO, C)
    for k in range(NB):
        a = 0 if k else 1
        act("kz", T.dl[:, _start(k) - 1 + a:_start(k) + 17], T.pat[:, a:18], F.Copy, "pat0 pat1 pat2 dl0 dl1 dl2", "dk%d" % k)
    act("kz", T.dl[:, TOT - 1:TOT], T.pat[:, 0:1], F.Copy, "pat0 dl2", "dk")
    quant_x(0, "l")
    mask("h")
    signed("l")
    fill("q1", T.cum[:, 0:1], 0.0, "cum0")

    for t in range(3):
        nbulk = send_state(t, False)
        if t == 0:
            unit(0)
        score(t, "sa", 4, 0, 0, LO + 16 * MINE["h"])
        score(t, "sb", 1, 0, 0, C)
        score(t, "s1", 2, 1, 0, C)
        step = {"mask": mask, "hold": hold, "compare": compare, "count": count, "wanted": wanted, "sums": sums, "counted": counted,
                "owned": owned, "kept": kept, "n1": n1, "n2": n2, "n16": n16, "name": name, "m16": m16, "addends": addends,
                "last": last, "ad": ad, "runs": runs, "v1": v1, "v2": v2, "a16": a16, "push": push, "places": places,
                "scatter": scatter, "oext": oext, "olist": olist,
                "table": lambda h, q: table(t, h, q), "send": lambda h: send(t, h), "shifted": lambda h: shifted(t, h),
                "mix": lambda h: mix(t, h), "loads": lambda: loads(t), "unpack": lambda: unpack(t, nbulk),
                "once": lambda i: t == 0 and once(i), "unpacker": lambda b: t == 0 and unpacker(b),
                "vtile": lambda: t == 2 and quant("qu", T.vc[:], T.vs[:], T.vt[:], "vt", "vq")}
        for w in ORDER:
            n, *arg = w.split(".")
            step[n](*[int(x) if x.isdigit() else x for x in arg])
        if t == 2:
            dma("y", "sto", T.od[:], T.orow[0:128:16, :], "orow")
        for w in LAYER:
            n, h = w[0], w[1]
            if n == "g":
                gather(t, h, int(w[2]), w[3])
            elif n == "q":
                quant_z(h)
            elif n == "z":
                z32(h, int(w[2]), w[3])
            elif n == "a":
                add(t, h, int(w[2]))
            elif n == "x":
                state(t, h, int(w[2]), w[3])
            elif n == "Q":
                quant_x(t + 1, h)
                if h == "h" and t < 2:
                    score(t + 1, "sh", 0, 0, LO, C)
                elif h == "h":
                    mm("sh", 0, T.vc[:], T.vs[:], T.xc3[:, LO:C], T.xs3[:, LO:C], "vq xq3h", n=C - LO)
            elif t < 2:
                mask(h)
            else:
                act("xsh", T.ysb[:, LO:C], bank(0, C - LO), F.Copy, "ps0", "ysbh")

    mm("sa", 4, T.vc[:], T.vs[:], T.xc3[:, 0:LO], T.xs3[:, 0:LO], "vq xq3l", n=LO)
    dma("y", "sto", T.oc[:], T.xc3[:].bitcast(u8), "xq3l xq3h")
    cp("sml", T.ysb[:, 0:LO], bank(4, LO), "ps4", "ysbl")
    dma("y", "sto", T.y[:], T.ysb[:], "ysbl ysbh")
    for k in range(4):
        dma("s", "sts", T.osc[4 * k:4 * k + 4, :], T.xs3[32 * k:32 * k + 4, :], "xq3l xq3h")
    _emit(g, T, ops)
    g.wait_ge(T.sem.out, sent[0])
